import numpy as np
import ml_dtypes


def mxq(x, axis, fmt="e4m3"):
    dtype, down = {"e4m3": (ml_dtypes.float8_e4m3fn, 7), "e5m2": (ml_dtypes.float8_e5m2, 14)}[fmt]
    v = np.moveaxis(np.asarray(x, np.float32).astype(ml_dtypes.bfloat16).astype(np.float64), axis, -1)
    blocks = v.reshape(v.shape[:-1] + (-1, 32))
    amax = np.abs(blocks).max(-1, keepdims=True)
    byte = np.maximum(np.where(amax > 0, np.frexp(amax)[1] - 1 + 127, 0) - down, 1)
    scale = np.exp2(byte - 127.0)
    codes = (blocks / scale).astype(np.float32).astype(dtype).astype(np.float64)
    return np.moveaxis((codes * scale).reshape(v.shape), -1, axis)


WIDE = False


def mx_kscale(k):
    if not WIDE:
        return np.ones(k)
    levels = np.array([10, -10, 5, -5, 0])
    if k % 512:
        return np.exp2(np.random.permutation(np.resize(levels, k // 32))).repeat(32)
    a = np.empty((k // 512, 16))
    for p in range(k // 512):
        a[p, :8] = np.random.permutation(np.resize(levels, 8))
        for g in range(8):
            far = levels[np.abs(levels - a[p, g]) >= 10]
            a[p, g + 8] = far[np.random.randint(len(far))]
    return np.exp2(a.ravel()).repeat(32)


def f64(x):
    return np.asarray(x).astype(np.float64)


def striped(idx):
    return np.tile(idx.reshape(-1, 16).T, (8, 1)).astype(np.uint16)


def unstriped(offs):
    return offs[:16].T.reshape(-1).astype(np.int64)


E2M1 = np.array([0.0, 0.5, 1.0, 1.5, 2.0, 3.0, 4.0, 6.0, -0.0, -0.5, -1.0, -1.5, -2.0, -3.0, -4.0, -6.0])


def pack_weight(w, fmt):
    k, n = w.shape
    w = f64(np.asarray(w, np.float32).astype(ml_dtypes.bfloat16)).reshape(k // 32, 32, n)
    amax = np.abs(w).max(1)
    if fmt == "e4m3":
        byte = np.frexp(amax)[1] - 1 + 127 - 7
    else:
        mant, ex = np.frexp(amax / 6.0)
        byte = np.where(mant > 0.5, ex, ex - 1) + 127
    byte = np.clip(np.where(amax > 0, byte, 1), 1, 254)
    scaled = (w * np.exp2(127.0 - byte)[:, None, :]).reshape(k, n).astype(np.float32)
    by_word = np.ascontiguousarray(scaled.reshape(k // 512, 128, 4, n).transpose(0, 1, 3, 2))
    if fmt == "e4m3":
        words = by_word.astype(ml_dtypes.float8_e4m3fn).view(np.uint8)
    else:
        c = by_word.astype(ml_dtypes.float4_e2m1fn).view(np.uint8) & 0xF
        words = (c[..., 0::2] | (c[..., 1::2] << 4)).reshape(k // 512, 128, 2 * n)
    return np.ascontiguousarray(words), np.ascontiguousarray(byte.astype(np.uint8).reshape(k // 512, 16, n))


def unpack_weight(words, scales, fmt):
    g, _, n = scales.shape
    words = np.ascontiguousarray(words).reshape(g, 128, n, -1)
    if fmt == "e4m3":
        vals = words.view(ml_dtypes.float8_e4m3fn).astype(np.float64)
    else:
        nib = np.empty((g, 128, n, 4), np.uint8)
        nib[..., 0::2] = words & 0xF
        nib[..., 1::2] = words >> 4
        vals = E2M1[nib]
    vals = vals * np.repeat(np.exp2(scales.astype(np.float64) - 127.0), 8, axis=1)[..., None]
    return vals.transpose(0, 1, 3, 2).reshape(g * 512, n)


def gelu(v):
    return 0.5 * v * (1.0 + np.tanh(np.sqrt(2.0 / np.pi) * (v + 0.044715 * v**3)))


def bf(x):
    return np.asarray(x, np.float32).astype(ml_dtypes.bfloat16)


def planes(Y):
    n, m = Y.shape
    b = f64(bf(Y)).reshape(n // 32, 32, m)
    amax = np.abs(b).max(1)
    byte = np.clip(np.where(amax > 0, np.frexp(amax)[1] - 1 + 127 - 7, 1), 1, 254)
    codes = (b * np.exp2(127.0 - byte)[:, None, :]).reshape(n, m).astype(np.float32).astype(ml_dtypes.float8_e4m3fn).view(np.uint8)
    words = codes.reshape(n // 512, 128, 4, m).transpose(0, 1, 3, 2)
    return np.ascontiguousarray(words), np.ascontiguousarray(byte.astype(np.uint8).reshape(n // 512, 16, m))


K, H, N, T, S, P = 1536, 512, 1024, 4096, 1024, 512

def setup_inputs():
    n = np.random.standard_normal
    s = mx_kscale(K)[:, None]
    u = mx_kscale(H)[:, None]
    d = {}
    d["tab_words"], d["tab_scales"] = pack_weight(n((K, T)) * s, "e4m3")
    d["offs"] = striped(np.random.permutation(T)[:S])
    d["pos1"] = striped(np.random.permutation(S)[:P])
    d["pos2"] = striped(np.random.permutation(S)[:P])
    spread = np.exp(0.5 * n(H))[None, :]
    d["w1"] = (2.5 * n((K, H)) * spread / s / K**0.5).astype(np.float32)
    d["w2_words"], d["w2_scales"] = pack_weight(0.8 * n((K, H)) / s / K**0.5, "e2m1")
    d["gain"] = (u[:, 0] * np.exp(0.3 * n(H))).astype(np.float32)
    size = np.exp(0.8 * n(N))
    d["w3"] = (0.5 * n((H, N)) * size[None, :] / u / H**0.5).astype(np.float32)
    d["lowest"] = ((n((N, S)) - 0.5) * size[:, None]).astype(np.float32)
    return d

def reference(tab_words, tab_scales, offs, pos1, pos2, w1, w2_words, w2_scales, gain, w3, lowest):
    v = unpack_weight(tab_words, tab_scales, "e4m3")[:, unstriped(offs)]
    a = mxq(f64(w1), 0, "e4m3").T @ v
    b = unpack_weight(w2_words, w2_scales, "e2m1").T @ v
    root = np.sqrt(np.abs(a))
    h = (root - b) * f64(gain)[:, None]
    hq = mxq(h, 0, "e4m3")
    level = mxq(f64(w3), 0, "e4m3").T @ hq
    level = np.maximum(level, f64(lowest))
    y = np.abs(level[:, unstriped(pos1)] + level[:, unstriped(pos2)])
    words, scales = planes(y)
    return y, words, scales

@@ -1,0 +1,282 @@
+from contextlib import ExitStack
+
+import concourse.mybir as mybir
+
+K, H, N, T, S, M = 1536, 512, 1024, 4096, 1024, 512
+FLOPS = 2 * K * H * S * 2 + 2 * H * N * S
+
+F32 = mybir.dt.float32
+BF16 = mybir.dt.bfloat16
+I32 = mybir.dt.int32
+U32 = mybir.dt.uint32
+U16 = mybir.dt.uint16
+U8 = mybir.dt.uint8
+FP8X4 = mybir.dt.float8_e4m3fn_x4
+FP4X4 = mybir.dt.float4_e2m1fn_x4
+ACT = mybir.ActivationFunctionType
+ALU = mybir.AluOpType
+
+P = 128
+PACK = 4
+K_PASS = P * PACK
+PASSES = K // K_PASS
+GROUPS = N // K_PASS
+HALF = 512
+QUARTER = 256
+MOVED_ROWS = 112
+
+
+def tile_list_pasta_humidity_features_kernel(
+    tc, tab_words, tab_scales, offs, pos1, pos2, w1, w2_words, w2_scales, gain, w3, lowest, out_0, out_1, out_2
+):
+    nc = tc.nc
+    with ExitStack() as ctx:
+        keep = ctx.enter_context(tc.tile_pool(name="keep", bufs=1))
+        ring = ctx.enter_context(tc.tile_pool(name="ring", bufs=2))
+        psum = ctx.enter_context(tc.psum_pool(name="psum", bufs=1))
+
+        def bank(b, shape):
+            return psum.tile(shape, F32, name="bank%d" % b, tag="bank%d" % b)
+
+        scale_window = keep.tile([P, T], U8, name="scale_window", align_bytes=64)
+        nc.vector.memset(scale_window[:].bitcast(I32), 0)
+        w2s_raw = keep.tile([P, PASSES, H], U8, name="w2s_raw", align_bytes=64)
+        nc.vector.memset(w2s_raw[:].bitcast(I32), 0)
+        moved = [keep.tile([P, S], U8, name="moved%d" % a, align_bytes=64) for a in range(1, PASSES)]
+        for plane in moved:
+            nc.vector.memset(plane[:].bitcast(I32), 0)
+
+        offs_t = keep.tile([P, S // 16], U16, name="offs_t")
+        nc.sync.dma_start(offs_t[:], offs)
+        w2w_raw = keep.tile([P, PASSES, 2 * H], U8, name="w2w_raw", align_bytes=64)
+        nc.sync.dma_start(w2w_raw[:].bitcast(I32), w2_words.rearrange("a p n -> p a n").bitcast(I32))
+        for q in range(4):
+            nc.gpsimd.dma_start(
+                scale_window[32 * q : 32 * q + 4 * PASSES, :].bitcast(I32),
+                tab_scales[:, 4 * q : 4 * q + 4, :].bitcast(I32),
+            )
+        for q in range(4):
+            nc.gpsimd.dma_start(
+                w2s_raw[32 * q : 32 * q + 4, :, :].bitcast(I32),
+                w2_scales[:, 4 * q : 4 * q + 4, :].rearrange("a r n -> r a n").bitcast(I32),
+            )
+        word_window = []
+        for a in range(PASSES):
+            win = keep.tile([P, T], I32, name="word_window%d" % a, tag="wide", bufs=PASSES, align_bytes=64)
+            nc.sync.dma_start(win[:], tab_words[a].rearrange("p t i -> p (t i)").bitcast(I32))
+            word_window.append(win)
+        gain_t = keep.tile([P, PACK], F32, name="gain_t")
+        nc.sync.dma_start(gain_t[:], gain.rearrange("(p t) -> p t", t=PACK))
+        w1_raw = []
+        for a in range(PASSES - 1):
+            raw = keep.tile([P, PACK, H], F32, name="w1_raw%d" % a, tag="rows", bufs=2)
+            nc.sync.dma_start(raw[:], w1[a * K_PASS : (a + 1) * K_PASS, :].rearrange("(p j) c -> p j c", j=PACK))
+            w1_raw.append(raw)
+        w1_last = []
+        for u in range(2):
+            raw = keep.tile([P, PACK, H // 2], F32, name="w1_last%d" % u)
+            nc.sync.dma_start(
+                raw[:],
+                w1[K - K_PASS : K, u * (H // 2) : (u + 1) * (H // 2)].rearrange("(p j) c -> p j c", j=PACK),
+            )
+            w1_last.append(raw)
+        pos1_t = keep.tile([P, M // 16], U16, name="pos1_t")
+        pos2_t = keep.tile([P, M // 16], U16, name="pos2_t")
+        w3_raw, level = [], []
+        for g in range(GROUPS):
+            raw = keep.tile([P, PACK, K_PASS], F32, name="w3_raw%d" % g)
+            nc.sync.dma_start(raw[:], w3[:, g * K_PASS : (g + 1) * K_PASS].rearrange("(p j) c -> p j c", j=PACK))
+            w3_raw.append(raw)
+            rows = lowest[g * K_PASS : (g + 1) * K_PASS, :].rearrange("(p t) s -> p t s", t=PACK)
+            level.append([])
+            for t in range(PACK):
+                lv = keep.tile([P, S], F32, name="level%d_%d" % (g, t))
+                nc.sync.dma_start(lv[:], rows[:, t, :])
+                level[g].append(lv)
+            if g == 0:
+                nc.sync.dma_start(pos1_t[:], pos1)
+                nc.sync.dma_start(pos2_t[:], pos2)
+
+        w2w = keep.tile([P, PASSES, 2 * H], U8, name="w2w", align_bytes=64)
+        nc.vector.tensor_copy(
+            out=w2w[:].rearrange("p a (t m e) -> p a t m e", t=PACK, e=2),
+            in_=w2w_raw[:].rearrange("p a (m t e) -> p a t m e", t=PACK, e=2),
+        )
+        picked_scales = keep.tile([P, S], U8, name="picked_scales", align_bytes=64)
+        nc.vector.tensor_copy(picked_scales[:], scale_window[:].indirect(offs_t[:]))
+        for a in range(1, PASSES):
+            nc.gpsimd.dma_start(
+                moved[a - 1][0:MOVED_ROWS, :].bitcast(I32),
+                picked_scales[4 * a : 4 * a + MOVED_ROWS, :].bitcast(I32),
+            )
+        v_scales = [picked_scales] + moved
+        w2s = keep.tile([P, PASSES, H], U8, name="w2s", align_bytes=64)
+        v_words = []
+        for a in range(PASSES):
+            words = keep.tile([P, S], U32, name="v_words%d" % a, align_bytes=64)
+            window = word_window[a][:].bitcast(U32)
+            if a < PASSES - 1:
+                nc.vector.tensor_copy(words[:], window.indirect(offs_t[:]))
+            else:
+                for hf in range(2):
+                    nc.vector.tensor_copy(
+                        words[:, hf * HALF : (hf + 1) * HALF],
+                        window.indirect(offs_t[:, hf * HALF // 16 : (hf + 1) * HALF // 16]),
+                    )
+            v_words.append(words)
+            if a == 0:
+                nc.vector.tensor_copy(
+                    out=w2s[:].rearrange("p a (t m) -> p a t m", t=PACK),
+                    in_=w2s_raw[:].rearrange("p a (m t) -> p a t m", t=PACK),
+                )
+
+        b_banks = [[bank(PACK * hf + t, [P, HALF]) for t in range(PACK)] for hf in range(2)]
+        for a in range(PASSES):
+            for hf in range(2):
+                cols = slice(hf * HALF, (hf + 1) * HALF)
+                for t in range(PACK):
+                    nc.tensor.matmul_mx(
+                        out=b_banks[hf][t][:],
+                        lhsT=w2w[:, a, 2 * P * t : 2 * P * (t + 1)].bitcast(FP4X4),
+                        lhsT_scale=w2s[:, a, P * t : P * (t + 1)],
+                        rhs=v_words[a][:, cols].bitcast(FP8X4),
+                        rhs_scale=v_scales[a][:, cols],
+                        start=(a == 0),
+                        stop=(a == PASSES - 1),
+                    )
+        gain_b = keep.tile([P, PACK, S], F32, name="gain_b", tag="wide", bufs=PASSES, align_bytes=64)
+        for hf in range(2):
+            for t in range(PACK):
+                nc.scalar.activation(
+                    gain_b[:, t, hf * HALF : (hf + 1) * HALF], b_banks[hf][t][:], ACT.Copy, scale=gain_t[:, t : t + 1]
+                )
+
+        w1_codes, w1_scales = [], []
+        for a in range(PASSES):
+            rounded = ring.tile([P, PACK * H], BF16, name="w1_rounded", align_bytes=64)
+            dealt = rounded[:].rearrange("p (t m j) -> p m j t", t=PACK, j=PACK)
+            codes = keep.tile([P, H], U32, name="w1_codes%d" % a, align_bytes=64)
+            scales = keep.tile([P, H], U8, name="w1_scales%d" % a, align_bytes=64)
+            if a < PASSES - 1:
+                nc.vector.tensor_copy(out=dealt, in_=w1_raw[a][:].rearrange("p j (m t) -> p m j t", t=PACK))
+                nc.vector.quantize_mx(out=codes[:].bitcast(FP8X4), scales=scales[:], in_=rounded[:])
+            else:
+                for u in range(2):
+                    nc.vector.tensor_copy(
+                        out=dealt[:, u * (P // 2) : (u + 1) * (P // 2), :, :],
+                        in_=w1_last[u][:].rearrange("p j (m t) -> p m j t", t=PACK),
+                    )
+                for t in range(PACK):
+                    nc.vector.quantize_mx(
+                        out=codes[:, t * P : (t + 1) * P].bitcast(FP8X4),
+                        scales=scales[:, t * P : (t + 1) * P],
+                        in_=rounded[:, t * K_PASS : (t + 1) * K_PASS],
+                    )
+            w1_codes.append(codes)
+            w1_scales.append(scales)
+
+        a_banks = []
+        for hf in range(2):
+            cols = slice(hf * HALF, (hf + 1) * HALF)
+            a_banks.append([bank(PACK * hf + t, [P, HALF]) for t in range(PACK)])
+            for a in range(PASSES):
+                for t in range(PACK):
+                    nc.tensor.matmul_mx(
+                        out=a_banks[hf][t][:],
+                        lhsT=w1_codes[a][:, P * t : P * (t + 1)].bitcast(FP8X4),
+                        lhsT_scale=w1_scales[a][:, P * t : P * (t + 1)],
+                        rhs=v_words[a][:, cols].bitcast(FP8X4),
+                        rhs_scale=v_scales[a][:, cols],
+                        start=(a == 0),
+                        stop=(a == PASSES - 1),
+                    )
+
+        w3_codes = keep.tile([P, N], U32, name="w3_codes", align_bytes=64)
+        w3_scales = keep.tile([P, N], U8, name="w3_scales", align_bytes=64)
+
+        def quantise_w3(g, copy):
+            rounded = ring.tile([P, PACK * K_PASS], BF16, name="w3_rounded", align_bytes=64)
+            copy(
+                out=rounded[:].rearrange("p (t m j) -> p m j t", t=PACK, j=PACK),
+                in_=w3_raw[g][:].rearrange("p j (m t) -> p m j t", t=PACK),
+            )
+            cols = slice(g * K_PASS, (g + 1) * K_PASS)
+            nc.vector.quantize_mx(out=w3_codes[:, cols].bitcast(FP8X4), scales=w3_scales[:, cols], in_=rounded[:])
+
+        quantise_w3(0, nc.vector.tensor_copy)
+
+        h_codes = keep.tile([P, S], U32, name="h_codes", align_bytes=64)
+        h_scales = keep.tile([P, S], U8, name="h_scales", align_bytes=64)
+
+        def second_product(out, g, t, cols):
+            wcols = slice(g * K_PASS + t * P, g * K_PASS + (t + 1) * P)
+            nc.tensor.matmul_mx(
+                out=out,
+                lhsT=w3_codes[:, wcols].bitcast(FP8X4),
+                lhsT_scale=w3_scales[:, wcols],
+                rhs=h_codes[:, cols].bitcast(FP8X4),
+                rhs_scale=h_scales[:, cols],
+                start=True,
+                stop=True,
+            )
+
+        for qt in range(S // QUARTER):
+            hf, part = divmod(qt, 2)
+            cols = slice(qt * QUARTER, (qt + 1) * QUARTER)
+            h_rows = ring.tile([P, PACK, QUARTER], F32, name="h_rows")
+            for t in range(PACK):
+                size = ring.tile([P, QUARTER], F32, name="size")
+                nc.scalar.activation(size[:], a_banks[hf][t][:, part * QUARTER : (part + 1) * QUARTER], ACT.Abs)
+                root = ring.tile([P, QUARTER], F32, name="root", bufs=8)
+                nc.scalar.activation(root[:], size[:], ACT.Sqrt)
+                nc.vector.scalar_tensor_tensor(
+                    h_rows[:, t, :], root[:], gain_t[:, t : t + 1], gain_b[:, t, cols], ALU.mult, ALU.subtract
+                )
+            h_rounded = ring.tile([P, PACK * QUARTER], BF16, name="h_rounded", align_bytes=64)
+            copy = nc.vector.tensor_copy if hf == 0 else nc.scalar.copy
+            copy(
+                out=h_rounded[:].rearrange("p (c i t) -> p c t i", i=4, t=PACK),
+                in_=h_rows[:].rearrange("p t (c i) -> p c t i", i=4),
+            )
+            nc.vector.quantize_mx(out=h_codes[:, cols].bitcast(FP8X4), scales=h_scales[:, cols], in_=h_rounded[:])
+            for pair in range(2):
+                both = bank(2 * part + pair, [P, 2, QUARTER])
+                for e in range(2):
+                    second_product(both[:, e, :], 0, 2 * pair + e, cols)
+                for e in range(2):
+                    lv = level[0][2 * pair + e]
+                    nc.vector.tensor_tensor(lv[:, cols], both[:, e, :], lv[:, cols], ALU.max)
+
+        quantise_w3(1, nc.scalar.copy)
+
+        for g in range(GROUPS):
+            y = keep.tile([P, PACK, M], F32, name="y%d" % g, tag="rows", bufs=2)
+            y_rows = out_0[g * K_PASS : (g + 1) * K_PASS, :].rearrange("(p t) m -> p t m", t=PACK)
+            for t in range(PACK):
+                lv = level[g][t]
+                if g > 0:
+                    for hf in range(2):
+                        cols = slice(hf * HALF, (hf + 1) * HALF)
+                        acc = bank((2 * t + hf + PACK) % 8, [P, HALF])
+                        second_product(acc[:], g, t, cols)
+                        nc.vector.tensor_tensor(lv[:, cols], acc[:], lv[:, cols], ALU.max)
+                core = ring.tile([P, M], F32, name="core")
+                nc.vector.tensor_copy(core[:], lv[:].indirect(pos1_t[:]))
+                pair_sum = ring.tile([P, M], F32, name="pair_sum")
+                nc.vector.tensor_tensor(pair_sum[:], lv[:].indirect(pos2_t[:]), core[:], ALU.add)
+                nc.scalar.activation(y[:, t, :], pair_sum[:], ACT.Abs)
+                nc.sync.dma_start(y_rows[:, t, :], y[:, t, :])
+            y_rounded = ring.tile([P, PACK * M], BF16, name="y_rounded", align_bytes=64)
+            copy = nc.scalar.copy if g == 0 else nc.vector.tensor_copy
+            copy(
+                out=y_rounded[:].rearrange("p (c i t) -> p c t i", i=4, t=PACK),
+                in_=y[:].rearrange("p t (c i) -> p c t i", i=4),
+            )
+            y_codes = ring.tile([P, M], U32, name="y_codes", align_bytes=64)
+            y_scales = ring.tile([P, M], U8, name="y_scales", align_bytes=64)
+            nc.vector.quantize_mx(out=y_codes[:].bitcast(FP8X4), scales=y_scales[:], in_=y_rounded[:])
+            nc.sync.dma_start(out_1[g].rearrange("p m t -> p (m t)").bitcast(I32), y_codes[:].bitcast(I32))
+            for q in range(4):
+                nc.sync.dma_start(
+                    out_2[g, 4 * q : 4 * q + 4, :].bitcast(I32), y_scales[32 * q : 32 * q + 4, :].bitcast(I32)
+                )

@@ -23,7 +23,9 @@ PASSES = K // K_PASS
 GROUPS = N // K_PASS
 HALF = 512
 QUARTER = 256
-MOVED_ROWS = 112
+QUADRANT = 32
+SPARE = QUADRANT - 4 * PASSES
+MOVED_ROWS = 3 * QUADRANT + 4
 
 
 def tile_list_pasta_humidity_features_kernel(
@@ -38,97 +40,91 @@ def tile_list_pasta_humidity_features_kernel(
         def bank(b, shape):
             return psum.tile(shape, F32, name="bank%d" % b, tag="bank%d" % b)
 
-        scale_window = keep.tile([P, T], U8, name="scale_window", align_bytes=64)
-        nc.vector.memset(scale_window[:].bitcast(I32), 0)
+        def slot(tag, shape, dtype, name):
+            return keep.tile(shape, dtype, name=name, tag=tag, align_bytes=64)
+
+        scale_window = slot("slot_a", [P, T], U8, "scale_window")
         w2s_raw = keep.tile([P, PASSES, H], U8, name="w2s_raw", align_bytes=64)
         nc.vector.memset(w2s_raw[:].bitcast(I32), 0)
-        moved = [keep.tile([P, S], U8, name="moved%d" % a, align_bytes=64) for a in range(1, PASSES)]
-        for plane in moved:
-            nc.vector.memset(plane[:].bitcast(I32), 0)
+        for q in range(4):
+            engine = nc.vector if q % 2 == 0 else nc.gpsimd
+            engine.memset(scale_window[QUADRANT * q : QUADRANT * q + SPARE, :].bitcast(I32), 0)
+        v_scales = [keep.tile([P, S], U8, name="v_scales%d" % a, align_bytes=64) for a in range(PASSES)]
+        for plane in v_scales:
+            nc.gpsimd.memset(plane[:].bitcast(I32), 0)
 
         offs_t = keep.tile([P, S // 16], U16, name="offs_t")
         nc.sync.dma_start(offs_t[:], offs)
-        w2w_raw = keep.tile([P, PASSES, 2 * H], U8, name="w2w_raw", align_bytes=64)
-        nc.sync.dma_start(w2w_raw[:].bitcast(I32), w2_words.rearrange("a p n -> p a n").bitcast(I32))
         for q in range(4):
-            nc.gpsimd.dma_start(
-                scale_window[32 * q : 32 * q + 4 * PASSES, :].bitcast(I32),
+            nc.sync.dma_start(
+                scale_window[QUADRANT * q + SPARE : QUADRANT * (q + 1), :].bitcast(I32),
                 tab_scales[:, 4 * q : 4 * q + 4, :].bitcast(I32),
             )
+
+        def load_words(a, tag):
+            window = slot(tag, [P, T], I32, "word_window%d" % a)
+            nc.sync.dma_start(window[:], tab_words[a].rearrange("p t i -> p (t i)").bitcast(I32))
+            return window
+
+        word_window = [load_words(0, "slot_d")]
         for q in range(4):
-            nc.gpsimd.dma_start(
-                w2s_raw[32 * q : 32 * q + 4, :, :].bitcast(I32),
+            nc.sync.dma_start(
+                w2s_raw[QUADRANT * q : QUADRANT * q + 4, :, :].bitcast(I32),
                 w2_scales[:, 4 * q : 4 * q + 4, :].rearrange("a r n -> r a n").bitcast(I32),
             )
-        word_window = []
-        for a in range(PASSES):
-            win = keep.tile([P, T], I32, name="word_window%d" % a, tag="wide", bufs=PASSES, align_bytes=64)
-            nc.sync.dma_start(win[:], tab_words[a].rearrange("p t i -> p (t i)").bitcast(I32))
-            word_window.append(win)
+        w2w_raw = slot("slot_b", [P, PASSES, 2 * H], U8, "w2w_raw")
+        nc.sync.dma_start(w2w_raw[:].bitcast(I32), w2_words.rearrange("a p n -> p a n").bitcast(I32))
+        pos1_t = keep.tile([P, M // 16], U16, name="pos1_t")
+        nc.sync.dma_start(pos1_t[:], pos1)
+        word_window.append(load_words(1, "slot_e"))
+        pos2_t = keep.tile([P, M // 16], U16, name="pos2_t")
+        nc.sync.dma_start(pos2_t[:], pos2)
         gain_t = keep.tile([P, PACK], F32, name="gain_t")
         nc.sync.dma_start(gain_t[:], gain.rearrange("(p t) -> p t", t=PACK))
+
+        picked_scales = slot("slot_c", [P, S], U8, "picked_scales")
+        nc.vector.tensor_copy(picked_scales[:], scale_window[:].indirect(offs_t[:]))
+        for a in range(PASSES):
+            nc.sync.dma_start(
+                v_scales[a][0:MOVED_ROWS, :].bitcast(I32),
+                picked_scales[SPARE + 4 * a : SPARE + 4 * a + MOVED_ROWS, :].bitcast(I32),
+            )
+        word_window.append(load_words(2, "slot_a"))
+        w2w = slot("slot_f", [P, PASSES, 2 * H], U8, "w2w")
+        for a in range(PASSES):
+            nc.vector.tensor_copy(
+                out=w2w[:, a, :].rearrange("p (t m e) -> p t m e", t=PACK, e=2),
+                in_=w2w_raw[:, a, :].rearrange("p (m t e) -> p t m e", t=PACK, e=2),
+            )
+        w2s = keep.tile([P, PASSES, H], U8, name="w2s", align_bytes=64)
+        for a in range(PASSES):
+            nc.vector.tensor_copy(
+                out=w2s[:, a, :].rearrange("p (t m) -> p t m", t=PACK),
+                in_=w2s_raw[:, a, :].rearrange("p (m t) -> p t m", t=PACK),
+            )
+
+        v_words = []
+        for a in range(PASSES):
+            window = word_window[a][:].bitcast(U32)
+            v_words.append([])
+            for hf in range(2):
+                words = slot("words%d_%d" % (a, hf), [P, HALF], U32, "v_words%d_%d" % (a, hf))
+                nc.vector.tensor_copy(words[:], window.indirect(offs_t[:, hf * HALF // 16 : (hf + 1) * HALF // 16]))
+                v_words[a].append(words)
+
         w1_raw = []
-        for a in range(PASSES - 1):
-            raw = keep.tile([P, PACK, H], F32, name="w1_raw%d" % a, tag="rows", bufs=2)
+        for a, tag in enumerate(["slot_b", "slot_d"]):
+            raw = slot(tag, [P, PACK, H], F32, "w1_raw%d" % a)
             nc.sync.dma_start(raw[:], w1[a * K_PASS : (a + 1) * K_PASS, :].rearrange("(p j) c -> p j c", j=PACK))
             w1_raw.append(raw)
         w1_last = []
-        for u in range(2):
-            raw = keep.tile([P, PACK, H // 2], F32, name="w1_last%d" % u)
+        for u, tag in enumerate(["slot_c", "slot_e"]):
+            raw = slot(tag, [P, PACK, H // 2], F32, "w1_last%d" % u)
             nc.sync.dma_start(
                 raw[:],
                 w1[K - K_PASS : K, u * (H // 2) : (u + 1) * (H // 2)].rearrange("(p j) c -> p j c", j=PACK),
             )
             w1_last.append(raw)
-        pos1_t = keep.tile([P, M // 16], U16, name="pos1_t")
-        pos2_t = keep.tile([P, M // 16], U16, name="pos2_t")
-        w3_raw, level = [], []
-        for g in range(GROUPS):
-            raw = keep.tile([P, PACK, K_PASS], F32, name="w3_raw%d" % g)
-            nc.sync.dma_start(raw[:], w3[:, g * K_PASS : (g + 1) * K_PASS].rearrange("(p j) c -> p j c", j=PACK))
-            w3_raw.append(raw)
-            rows = lowest[g * K_PASS : (g + 1) * K_PASS, :].rearrange("(p t) s -> p t s", t=PACK)
-            level.append([])
-            for t in range(PACK):
-                lv = keep.tile([P, S], F32, name="level%d_%d" % (g, t))
-                nc.sync.dma_start(lv[:], rows[:, t, :])
-                level[g].append(lv)
-            if g == 0:
-                nc.sync.dma_start(pos1_t[:], pos1)
-                nc.sync.dma_start(pos2_t[:], pos2)
-
-        w2w = keep.tile([P, PASSES, 2 * H], U8, name="w2w", align_bytes=64)
-        nc.vector.tensor_copy(
-            out=w2w[:].rearrange("p a (t m e) -> p a t m e", t=PACK, e=2),
-            in_=w2w_raw[:].rearrange("p a (m t e) -> p a t m e", t=PACK, e=2),
-        )
-        picked_scales = keep.tile([P, S], U8, name="picked_scales", align_bytes=64)
-        nc.vector.tensor_copy(picked_scales[:], scale_window[:].indirect(offs_t[:]))
-        for a in range(1, PASSES):
-            nc.gpsimd.dma_start(
-                moved[a - 1][0:MOVED_ROWS, :].bitcast(I32),
-                picked_scales[4 * a : 4 * a + MOVED_ROWS, :].bitcast(I32),
-            )
-        v_scales = [picked_scales] + moved
-        w2s = keep.tile([P, PASSES, H], U8, name="w2s", align_bytes=64)
-        v_words = []
-        for a in range(PASSES):
-            words = keep.tile([P, S], U32, name="v_words%d" % a, align_bytes=64)
-            window = word_window[a][:].bitcast(U32)
-            if a < PASSES - 1:
-                nc.vector.tensor_copy(words[:], window.indirect(offs_t[:]))
-            else:
-                for hf in range(2):
-                    nc.vector.tensor_copy(
-                        words[:, hf * HALF : (hf + 1) * HALF],
-                        window.indirect(offs_t[:, hf * HALF // 16 : (hf + 1) * HALF // 16]),
-                    )
-            v_words.append(words)
-            if a == 0:
-                nc.vector.tensor_copy(
-                    out=w2s[:].rearrange("p a (t m) -> p a t m", t=PACK),
-                    in_=w2s_raw[:].rearrange("p a (m t) -> p a t m", t=PACK),
-                )
 
         b_banks = [[bank(PACK * hf + t, [P, HALF]) for t in range(PACK)] for hf in range(2)]
         for a in range(PASSES):
@@ -139,12 +135,12 @@ def tile_list_pasta_humidity_features_kernel(
                         out=b_banks[hf][t][:],
                         lhsT=w2w[:, a, 2 * P * t : 2 * P * (t + 1)].bitcast(FP4X4),
                         lhsT_scale=w2s[:, a, P * t : P * (t + 1)],
-                        rhs=v_words[a][:, cols].bitcast(FP8X4),
+                        rhs=v_words[a][hf][:].bitcast(FP8X4),
                         rhs_scale=v_scales[a][:, cols],
                         start=(a == 0),
                         stop=(a == PASSES - 1),
                     )
-        gain_b = keep.tile([P, PACK, S], F32, name="gain_b", tag="wide", bufs=PASSES, align_bytes=64)
+        gain_b = keep.tile([P, PACK, S], F32, name="gain_b")
         for hf in range(2):
             for t in range(PACK):
                 nc.scalar.activation(
@@ -154,17 +150,17 @@ def tile_list_pasta_humidity_features_kernel(
         w1_codes, w1_scales = [], []
         for a in range(PASSES):
             rounded = ring.tile([P, PACK * H], BF16, name="w1_rounded", align_bytes=64)
-            dealt = rounded[:].rearrange("p (t m j) -> p m j t", t=PACK, j=PACK)
-            codes = keep.tile([P, H], U32, name="w1_codes%d" % a, align_bytes=64)
+            dealt = rounded[:].rearrange("p (u e m j) -> p u m j e", u=2, e=2, j=PACK)
+            codes = slot("w1_codes%d" % a, [P, H], U32, "w1_codes%d" % a)
             scales = keep.tile([P, H], U8, name="w1_scales%d" % a, align_bytes=64)
             if a < PASSES - 1:
-                nc.vector.tensor_copy(out=dealt, in_=w1_raw[a][:].rearrange("p j (m t) -> p m j t", t=PACK))
+                nc.vector.tensor_copy(out=dealt, in_=w1_raw[a][:].rearrange("p j (m u e) -> p u m j e", u=2, e=2))
                 nc.vector.quantize_mx(out=codes[:].bitcast(FP8X4), scales=scales[:], in_=rounded[:])
             else:
                 for u in range(2):
                     nc.vector.tensor_copy(
-                        out=dealt[:, u * (P // 2) : (u + 1) * (P // 2), :, :],
-                        in_=w1_last[u][:].rearrange("p j (m t) -> p m j t", t=PACK),
+                        out=dealt[:, :, u * (P // 2) : (u + 1) * (P // 2), :, :],
+                        in_=w1_last[u][:].rearrange("p j (m u e) -> p u m j e", u=2, e=2),
                     )
                 for t in range(PACK):
                     nc.vector.quantize_mx(
@@ -185,25 +181,39 @@ def tile_list_pasta_humidity_features_kernel(
                         out=a_banks[hf][t][:],
                         lhsT=w1_codes[a][:, P * t : P * (t + 1)].bitcast(FP8X4),
                         lhsT_scale=w1_scales[a][:, P * t : P * (t + 1)],
-                        rhs=v_words[a][:, cols].bitcast(FP8X4),
+                        rhs=v_words[a][hf][:].bitcast(FP8X4),
                         rhs_scale=v_scales[a][:, cols],
                         start=(a == 0),
                         stop=(a == PASSES - 1),
                     )
 
+        w3_raw, level = [], []
+        w3_tags = ["slot_a", "words0_1"]
+        level_tags = [["slot_f", "slot_d", "slot_c", "slot_e"], ["words1_1", "words2_1", "w1_codes2", "w1_codes1"]]
+        for g in range(GROUPS):
+            raw = slot(w3_tags[g], [P, PACK, K_PASS], F32, "w3_raw%d" % g)
+            nc.sync.dma_start(raw[:], w3[:, g * K_PASS : (g + 1) * K_PASS].rearrange("(p j) c -> p j c", j=PACK))
+            w3_raw.append(raw)
+            rows = lowest[g * K_PASS : (g + 1) * K_PASS, :].rearrange("(p t) s -> p t s", t=PACK)
+            level.append([])
+            for t in range(PACK):
+                lv = slot(level_tags[g][t], [P, S], F32, "level%d_%d" % (g, t))
+                nc.sync.dma_start(lv[:], rows[:, t, :])
+                level[g].append(lv)
+
         w3_codes = keep.tile([P, N], U32, name="w3_codes", align_bytes=64)
         w3_scales = keep.tile([P, N], U8, name="w3_scales", align_bytes=64)
 
-        def quantise_w3(g, copy):
-            rounded = ring.tile([P, PACK * K_PASS], BF16, name="w3_rounded", align_bytes=64)
+        def quantise_w3(g, copy, tag):
+            rounded = ring.tile([P, PACK * K_PASS], BF16, name="w3_rounded", tag=tag, align_bytes=64)
             copy(
-                out=rounded[:].rearrange("p (t m j) -> p m j t", t=PACK, j=PACK),
-                in_=w3_raw[g][:].rearrange("p j (m t) -> p m j t", t=PACK),
+                out=rounded[:].rearrange("p (u e m j) -> p u m j e", u=2, e=2, j=PACK),
+                in_=w3_raw[g][:].rearrange("p j (m u e) -> p u m j e", u=2, e=2),
             )
             cols = slice(g * K_PASS, (g + 1) * K_PASS)
             nc.vector.quantize_mx(out=w3_codes[:, cols].bitcast(FP8X4), scales=w3_scales[:, cols], in_=rounded[:])
 
-        quantise_w3(0, nc.vector.tensor_copy)
+        quantise_w3(0, nc.vector.tensor_copy, "w1_rounded")
 
         h_codes = keep.tile([P, S], U32, name="h_codes", align_bytes=64)
         h_scales = keep.tile([P, S], U8, name="h_scales", align_bytes=64)
@@ -223,7 +233,7 @@ def tile_list_pasta_humidity_features_kernel(
         for qt in range(S // QUARTER):
             hf, part = divmod(qt, 2)
             cols = slice(qt * QUARTER, (qt + 1) * QUARTER)
-            h_rows = ring.tile([P, PACK, QUARTER], F32, name="h_rows")
+            h_rows = ring.tile([P, PACK, QUARTER], F32, name="h_rows", align_bytes=64)
             for t in range(PACK):
                 size = ring.tile([P, QUARTER], F32, name="size")
                 nc.scalar.activation(size[:], a_banks[hf][t][:, part * QUARTER : (part + 1) * QUARTER], ACT.Abs)
@@ -233,7 +243,7 @@ def tile_list_pasta_humidity_features_kernel(
                     h_rows[:, t, :], root[:], gain_t[:, t : t + 1], gain_b[:, t, cols], ALU.mult, ALU.subtract
                 )
             h_rounded = ring.tile([P, PACK * QUARTER], BF16, name="h_rounded", align_bytes=64)
-            copy = nc.vector.tensor_copy if hf == 0 else nc.scalar.copy
+            copy = nc.vector.tensor_copy if qt == 0 else nc.scalar.copy
             copy(
                 out=h_rounded[:].rearrange("p (c i t) -> p c t i", i=4, t=PACK),
                 in_=h_rows[:].rearrange("p t (c i) -> p c t i", i=4),
@@ -247,36 +257,65 @@ def tile_list_pasta_humidity_features_kernel(
                     lv = level[0][2 * pair + e]
                     nc.vector.tensor_tensor(lv[:, cols], both[:, e, :], lv[:, cols], ALU.max)
 
-        quantise_w3(1, nc.scalar.copy)
+        quantise_w3(1, nc.scalar.copy, "h_rows")
 
-        for g in range(GROUPS):
-            y = keep.tile([P, PACK, M], F32, name="y%d" % g, tag="rows", bufs=2)
-            y_rows = out_0[g * K_PASS : (g + 1) * K_PASS, :].rearrange("(p t) m -> p t m", t=PACK)
-            for t in range(PACK):
-                lv = level[g][t]
-                if g > 0:
-                    for hf in range(2):
-                        cols = slice(hf * HALF, (hf + 1) * HALF)
-                        acc = bank((2 * t + hf + PACK) % 8, [P, HALF])
-                        second_product(acc[:], g, t, cols)
-                        nc.vector.tensor_tensor(lv[:, cols], acc[:], lv[:, cols], ALU.max)
-                core = ring.tile([P, M], F32, name="core")
-                nc.vector.tensor_copy(core[:], lv[:].indirect(pos1_t[:]))
-                pair_sum = ring.tile([P, M], F32, name="pair_sum")
-                nc.vector.tensor_tensor(pair_sum[:], lv[:].indirect(pos2_t[:]), core[:], ALU.add)
-                nc.scalar.activation(y[:, t, :], pair_sum[:], ACT.Abs)
-                nc.sync.dma_start(y_rows[:, t, :], y[:, t, :])
-            y_rounded = ring.tile([P, PACK * M], BF16, name="y_rounded", align_bytes=64)
-            copy = nc.scalar.copy if g == 0 else nc.vector.tensor_copy
+        y_tiles = [keep.tile([P, PACK, M], F32, name="y%d" % g) for g in range(GROUPS)]
+        y_rounded = [keep.tile([P, PACK * M], BF16, name="y_rounded%d" % g, align_bytes=64) for g in range(GROUPS)]
+        y_codes = [keep.tile([P, M], U32, name="y_codes%d" % g, align_bytes=64) for g in range(GROUPS)]
+        y_scales = [keep.tile([P, M], U8, name="y_scales%d" % g, align_bytes=64) for g in range(GROUPS)]
+
+        def raise_level(g, t):
+            lv = level[g][t]
+            for hf in range(2):
+                cols = slice(hf * HALF, (hf + 1) * HALF)
+                acc = bank((2 * t + hf + PACK) % 8, [P, HALF])
+                second_product(acc[:], g, t, cols)
+                nc.vector.tensor_tensor(lv[:, cols], acc[:], lv[:, cols], ALU.max)
+
+        def pick_core(g, t, m0, m1):
+            core = ring.tile([P, m1 - m0], F32, name="core", bufs=3)
+            nc.vector.tensor_copy(core[:], level[g][t][:].indirect(pos1_t[:, m0 // 16 : m1 // 16]))
+            return core
+
+        def planes(g, m0, m1, copy):
             copy(
-                out=y_rounded[:].rearrange("p (c i t) -> p c t i", i=4, t=PACK),
-                in_=y[:].rearrange("p t (c i) -> p c t i", i=4),
+                out=y_rounded[g][:, PACK * m0 : PACK * m1].rearrange("p (c i t) -> p c t i", i=4, t=PACK),
+                in_=y_tiles[g][:, :, m0:m1].rearrange("p t (c i) -> p c t i", i=4),
             )
-            y_codes = ring.tile([P, M], U32, name="y_codes", align_bytes=64)
-            y_scales = ring.tile([P, M], U8, name="y_scales", align_bytes=64)
-            nc.vector.quantize_mx(out=y_codes[:].bitcast(FP8X4), scales=y_scales[:], in_=y_rounded[:])
-            nc.sync.dma_start(out_1[g].rearrange("p m t -> p (m t)").bitcast(I32), y_codes[:].bitcast(I32))
-            for q in range(4):
-                nc.sync.dma_start(
-                    out_2[g, 4 * q : 4 * q + 4, :].bitcast(I32), y_scales[32 * q : 32 * q + 4, :].bitcast(I32)
-                )
+            nc.vector.quantize_mx(
+                out=y_codes[g][:, m0:m1].bitcast(FP8X4),
+                scales=y_scales[g][:, m0:m1],
+                in_=y_rounded[g][:, PACK * m0 : PACK * m1],
+            )
+            nc.sync.dma_start(
+                out_1[g, :, m0:m1, :].rearrange("p m t -> p (m t)").bitcast(I32), y_codes[g][:, m0:m1].bitcast(I32)
+            )
+            if m1 == M:
+                for q in range(4):
+                    queue = nc.sync if q % 2 == 0 else nc.scalar
+                    queue.dma_start(
+                        out_2[g, 4 * q : 4 * q + 4, :].bitcast(I32), y_scales[g][32 * q : 32 * q + 4, :].bitcast(I32)
+                    )
+
+        def add_surface(g, t, m0, m1, core):
+            pair_sum = ring.tile([P, m1 - m0], F32, name="pair_sum")
+            nc.vector.tensor_tensor(
+                pair_sum[:], level[g][t][:].indirect(pos2_t[:, m0 // 16 : m1 // 16]), core[:], ALU.add
+            )
+            nc.scalar.activation(y_tiles[g][:, t, m0:m1], pair_sum[:], ACT.Abs)
+            y_rows = out_0[g * K_PASS : (g + 1) * K_PASS, :].rearrange("(p t) m -> p t m", t=PACK)
+            nc.sync.dma_start(y_rows[:, t, m0:m1], y_tiles[g][:, t, m0:m1])
+            if t == PACK - 1:
+                planes(g, m0, m1, nc.vector.tensor_copy if (g == GROUPS - 1 and m1 == M) else nc.scalar.copy)
+
+        pieces = [(g, t, 0, M) for g in range(GROUPS) for t in range(PACK)][:-1]
+        pieces.extend([(GROUPS - 1, PACK - 1, 0, M // 2), (GROUPS - 1, PACK - 1, M // 2, M)])
+        waiting = None
+        for g, t, m0, m1 in pieces:
+            if g > 0 and m0 == 0:
+                raise_level(g, t)
+            core = pick_core(g, t, m0, m1)
+            if waiting is not None:
+                add_surface(*waiting)
+            waiting = (g, t, m0, m1, core)
+        add_surface(*waiting)

@@ -24,8 +24,7 @@ GROUPS = N // K_PASS
 HALF = 512
 QUARTER = 256
 QUADRANT = 32
-SPARE = QUADRANT - 4 * PASSES
-MOVED_ROWS = 3 * QUADRANT + 4
+MOVED_ROWS = 112
 
 
 def tile_list_pasta_humidity_features_kernel(
@@ -44,51 +43,56 @@ def tile_list_pasta_humidity_features_kernel(
             return keep.tile(shape, dtype, name=name, tag=tag, align_bytes=64)
 
         scale_window = slot("slot_a", [P, T], U8, "scale_window")
+        nc.gpsimd.memset(scale_window[:, : T // 2].bitcast(I32), 0)
+        nc.vector.memset(scale_window[:, T // 2 :].bitcast(I32), 0)
         w2s_raw = keep.tile([P, PASSES, H], U8, name="w2s_raw", align_bytes=64)
         nc.vector.memset(w2s_raw[:].bitcast(I32), 0)
-        for q in range(4):
-            engine = nc.vector if q % 2 == 0 else nc.gpsimd
-            engine.memset(scale_window[QUADRANT * q : QUADRANT * q + SPARE, :].bitcast(I32), 0)
-        v_scales = [keep.tile([P, S], U8, name="v_scales%d" % a, align_bytes=64) for a in range(PASSES)]
-        for plane in v_scales:
+        moved = [keep.tile([P, S], U8, name="moved%d" % a, align_bytes=64) for a in range(1, PASSES)]
+        for plane in moved:
             nc.gpsimd.memset(plane[:].bitcast(I32), 0)
-
-        offs_t = keep.tile([P, S // 16], U16, name="offs_t")
-        nc.sync.dma_start(offs_t[:], offs)
-        for q in range(4):
-            nc.sync.dma_start(
-                scale_window[QUADRANT * q + SPARE : QUADRANT * (q + 1), :].bitcast(I32),
-                tab_scales[:, 4 * q : 4 * q + 4, :].bitcast(I32),
-            )
 
         def load_words(a, tag):
             window = slot(tag, [P, T], I32, "word_window%d" % a)
             nc.sync.dma_start(window[:], tab_words[a].rearrange("p t i -> p (t i)").bitcast(I32))
             return window
 
+        def load_w1(a, tag):
+            raw = slot(tag, [P, PACK, H], F32, "w1_raw%d" % a)
+            nc.sync.dma_start(raw[:], w1[a * K_PASS : (a + 1) * K_PASS, :].rearrange("(p j) c -> p j c", j=PACK))
+            return raw
+
+        offs_t = keep.tile([P, S // 16], U16, name="offs_t")
+        nc.sync.dma_start(offs_t[:], offs)
         word_window = [load_words(0, "slot_d")]
+        for q in range(4):
+            nc.sync.dma_start(
+                scale_window[QUADRANT * q : QUADRANT * q + 4 * PASSES, :].bitcast(I32),
+                tab_scales[:, 4 * q : 4 * q + 4, :].bitcast(I32),
+            )
+        w2w_raw = keep.tile([P, PASSES, 2 * H], U8, name="w2w_raw", align_bytes=64)
+        nc.sync.dma_start(w2w_raw[:].bitcast(I32), w2_words.rearrange("a p n -> p a n").bitcast(I32))
+        pos1_t = keep.tile([P, M // 16], U16, name="pos1_t")
+        nc.sync.dma_start(pos1_t[:], pos1)
+        pos2_t = keep.tile([P, M // 16], U16, name="pos2_t")
+        nc.sync.dma_start(pos2_t[:], pos2)
+        gain_t = keep.tile([P, PACK], F32, name="gain_t")
+        nc.sync.dma_start(gain_t[:], gain.rearrange("(p t) -> p t", t=PACK))
+        word_window.append(load_words(1, "slot_e"))
         for q in range(4):
             nc.sync.dma_start(
                 w2s_raw[QUADRANT * q : QUADRANT * q + 4, :, :].bitcast(I32),
                 w2_scales[:, 4 * q : 4 * q + 4, :].rearrange("a r n -> r a n").bitcast(I32),
             )
-        w2w_raw = slot("slot_b", [P, PASSES, 2 * H], U8, "w2w_raw")
-        nc.sync.dma_start(w2w_raw[:].bitcast(I32), w2_words.rearrange("a p n -> p a n").bitcast(I32))
-        pos1_t = keep.tile([P, M // 16], U16, name="pos1_t")
-        nc.sync.dma_start(pos1_t[:], pos1)
-        word_window.append(load_words(1, "slot_e"))
-        pos2_t = keep.tile([P, M // 16], U16, name="pos2_t")
-        nc.sync.dma_start(pos2_t[:], pos2)
-        gain_t = keep.tile([P, PACK], F32, name="gain_t")
-        nc.sync.dma_start(gain_t[:], gain.rearrange("(p t) -> p t", t=PACK))
+        w1_raw = [load_w1(0, "slot_b")]
 
-        picked_scales = slot("slot_c", [P, S], U8, "picked_scales")
+        picked_scales = keep.tile([P, S], U8, name="picked_scales", align_bytes=64)
         nc.vector.tensor_copy(picked_scales[:], scale_window[:].indirect(offs_t[:]))
-        for a in range(PASSES):
+        for a in range(1, PASSES):
             nc.sync.dma_start(
-                v_scales[a][0:MOVED_ROWS, :].bitcast(I32),
-                picked_scales[SPARE + 4 * a : SPARE + 4 * a + MOVED_ROWS, :].bitcast(I32),
+                moved[a - 1][0:MOVED_ROWS, :].bitcast(I32),
+                picked_scales[4 * a : 4 * a + MOVED_ROWS, :].bitcast(I32),
             )
+        v_scales = [picked_scales] + moved
         word_window.append(load_words(2, "slot_a"))
         w2w = slot("slot_f", [P, PASSES, 2 * H], U8, "w2w")
         for a in range(PASSES):
@@ -103,28 +107,40 @@ def tile_list_pasta_humidity_features_kernel(
                 in_=w2s_raw[:, a, :].rearrange("p (m t) -> p t m", t=PACK),
             )
 
-        v_words = []
-        for a in range(PASSES):
+        def pick_words(a):
             window = word_window[a][:].bitcast(U32)
-            v_words.append([])
+            halves = []
             for hf in range(2):
                 words = slot("words%d_%d" % (a, hf), [P, HALF], U32, "v_words%d_%d" % (a, hf))
                 nc.vector.tensor_copy(words[:], window.indirect(offs_t[:, hf * HALF // 16 : (hf + 1) * HALF // 16]))
-                v_words[a].append(words)
+                halves.append(words)
+            return halves
 
-        w1_raw = []
-        for a, tag in enumerate(["slot_b", "slot_d"]):
-            raw = slot(tag, [P, PACK, H], F32, "w1_raw%d" % a)
-            nc.sync.dma_start(raw[:], w1[a * K_PASS : (a + 1) * K_PASS, :].rearrange("(p j) c -> p j c", j=PACK))
-            w1_raw.append(raw)
-        w1_last = []
-        for u, tag in enumerate(["slot_c", "slot_e"]):
-            raw = slot(tag, [P, PACK, H // 2], F32, "w1_last%d" % u)
-            nc.sync.dma_start(
-                raw[:],
-                w1[K - K_PASS : K, u * (H // 2) : (u + 1) * (H // 2)].rearrange("(p j) c -> p j c", j=PACK),
-            )
-            w1_last.append(raw)
+        w1_codes = [slot("w1_codes%d" % a, [P, H], U32, "w1_codes%d" % a) for a in range(PASSES)]
+        w1_scales = [keep.tile([P, H], U8, name="w1_scales%d" % a, align_bytes=64) for a in range(PASSES)]
+
+        def quantise_w1(a, tag, parts):
+            rounded = slot(tag, [P, PACK * H], BF16, "w1_rounded%d" % a)
+            dealt = rounded[:].rearrange("p (u e m j) -> p u m j e", u=2, e=2, j=PACK)
+            rows = w1_raw[a][:].rearrange("p j (m u e) -> p u m j e", u=2, e=2)
+            if parts == 1:
+                nc.vector.tensor_copy(out=dealt, in_=rows)
+            else:
+                for u in range(2):
+                    nc.vector.tensor_copy(out=dealt[:, u, :, :, :], in_=rows[:, u, :, :, :])
+            width = H // parts
+            for c0 in range(0, H, width):
+                nc.vector.quantize_mx(
+                    out=w1_codes[a][:, c0 : c0 + width].bitcast(FP8X4),
+                    scales=w1_scales[a][:, c0 : c0 + width],
+                    in_=rounded[:, PACK * c0 : PACK * (c0 + width)],
+                )
+
+        v_words = [pick_words(0), pick_words(1)]
+        w1_raw.append(load_w1(1, "slot_e"))
+        quantise_w1(0, "slot_g", 1)
+        w1_raw.append(load_w1(2, "slot_b"))
+        v_words.append(pick_words(2))
 
         b_banks = [[bank(PACK * hf + t, [P, HALF]) for t in range(PACK)] for hf in range(2)]
         for a in range(PASSES):
@@ -147,29 +163,8 @@ def tile_list_pasta_humidity_features_kernel(
                     gain_b[:, t, hf * HALF : (hf + 1) * HALF], b_banks[hf][t][:], ACT.Copy, scale=gain_t[:, t : t + 1]
                 )
 
-        w1_codes, w1_scales = [], []
-        for a in range(PASSES):
-            rounded = ring.tile([P, PACK * H], BF16, name="w1_rounded", align_bytes=64)
-            dealt = rounded[:].rearrange("p (u e m j) -> p u m j e", u=2, e=2, j=PACK)
-            codes = slot("w1_codes%d" % a, [P, H], U32, "w1_codes%d" % a)
-            scales = keep.tile([P, H], U8, name="w1_scales%d" % a, align_bytes=64)
-            if a < PASSES - 1:
-                nc.vector.tensor_copy(out=dealt, in_=w1_raw[a][:].rearrange("p j (m u e) -> p u m j e", u=2, e=2))
-                nc.vector.quantize_mx(out=codes[:].bitcast(FP8X4), scales=scales[:], in_=rounded[:])
-            else:
-                for u in range(2):
-                    nc.vector.tensor_copy(
-                        out=dealt[:, :, u * (P // 2) : (u + 1) * (P // 2), :, :],
-                        in_=w1_last[u][:].rearrange("p j (m u e) -> p u m j e", u=2, e=2),
-                    )
-                for t in range(PACK):
-                    nc.vector.quantize_mx(
-                        out=codes[:, t * P : (t + 1) * P].bitcast(FP8X4),
-                        scales=scales[:, t * P : (t + 1) * P],
-                        in_=rounded[:, t * K_PASS : (t + 1) * K_PASS],
-                    )
-            w1_codes.append(codes)
-            w1_scales.append(scales)
+        quantise_w1(1, "slot_h", 1)
+        quantise_w1(2, "slot_i", 2)
 
         a_banks = []
         for hf in range(2):
@@ -188,8 +183,8 @@ def tile_list_pasta_humidity_features_kernel(
                     )
 
         w3_raw, level = [], []
-        w3_tags = ["slot_a", "words0_1"]
-        level_tags = [["slot_f", "slot_d", "slot_c", "slot_e"], ["words1_1", "words2_1", "w1_codes2", "w1_codes1"]]
+        w3_tags = ["slot_g", "words0_1"]
+        level_tags = [["slot_a", "slot_f", "slot_e", "slot_b"], ["words1_1", "words2_1", "w1_codes2", "w1_codes1"]]
         for g in range(GROUPS):
             raw = slot(w3_tags[g], [P, PACK, K_PASS], F32, "w3_raw%d" % g)
             nc.sync.dma_start(raw[:], w3[:, g * K_PASS : (g + 1) * K_PASS].rearrange("(p j) c -> p j c", j=PACK))
@@ -213,7 +208,7 @@ def tile_list_pasta_humidity_features_kernel(
             cols = slice(g * K_PASS, (g + 1) * K_PASS)
             nc.vector.quantize_mx(out=w3_codes[:, cols].bitcast(FP8X4), scales=w3_scales[:, cols], in_=rounded[:])
 
-        quantise_w3(0, nc.vector.tensor_copy, "w1_rounded")
+        quantise_w3(0, nc.vector.tensor_copy, "w3_rounded")
 
         h_codes = keep.tile([P, S], U32, name="h_codes", align_bytes=64)
         h_scales = keep.tile([P, S], U8, name="h_scales", align_bytes=64)
@@ -234,16 +229,18 @@ def tile_list_pasta_humidity_features_kernel(
             hf, part = divmod(qt, 2)
             cols = slice(qt * QUARTER, (qt + 1) * QUARTER)
             h_rows = ring.tile([P, PACK, QUARTER], F32, name="h_rows", align_bytes=64)
+            size = ring.tile([P, PACK, QUARTER], F32, name="size")
             for t in range(PACK):
-                size = ring.tile([P, QUARTER], F32, name="size")
-                nc.scalar.activation(size[:], a_banks[hf][t][:, part * QUARTER : (part + 1) * QUARTER], ACT.Abs)
-                root = ring.tile([P, QUARTER], F32, name="root", bufs=8)
-                nc.scalar.activation(root[:], size[:], ACT.Sqrt)
+                nc.scalar.activation(size[:, t, :], a_banks[hf][t][:, part * QUARTER : (part + 1) * QUARTER], ACT.Abs)
+            root = ring.tile([P, PACK, QUARTER], F32, name="root")
+            for t in range(0, PACK, 2):
+                nc.scalar.activation(root[:, t : t + 2, :], size[:, t : t + 2, :], ACT.Sqrt)
+            for t in range(PACK):
                 nc.vector.scalar_tensor_tensor(
-                    h_rows[:, t, :], root[:], gain_t[:, t : t + 1], gain_b[:, t, cols], ALU.mult, ALU.subtract
+                    h_rows[:, t, :], root[:, t, :], gain_t[:, t : t + 1], gain_b[:, t, cols], ALU.mult, ALU.subtract
                 )
             h_rounded = ring.tile([P, PACK * QUARTER], BF16, name="h_rounded", align_bytes=64)
-            copy = nc.vector.tensor_copy if qt == 0 else nc.scalar.copy
+            copy = nc.vector.tensor_copy if qt in (0, S // QUARTER - 1) else nc.scalar.copy
             copy(
                 out=h_rounded[:].rearrange("p (c i t) -> p c t i", i=4, t=PACK),
                 in_=h_rows[:].rearrange("p t (c i) -> p c t i", i=4),
@@ -311,9 +308,9 @@ def tile_list_pasta_humidity_features_kernel(
         pieces = [(g, t, 0, M) for g in range(GROUPS) for t in range(PACK)][:-1]
         pieces.extend([(GROUPS - 1, PACK - 1, 0, M // 2), (GROUPS - 1, PACK - 1, M // 2, M)])
         waiting = None
-        for g, t, m0, m1 in pieces:
-            if g > 0 and m0 == 0:
-                raise_level(g, t)
+        for i, (g, t, m0, m1) in enumerate(pieces):
+            if PACK <= i + 1 < GROUPS * PACK:
+                raise_level(*divmod(i + 1, PACK))
             core = pick_core(g, t, m0, m1)
             if waiting is not None:
                 add_surface(*waiting)

@@ -21,9 +21,14 @@ PACK = 4
 K_PASS = P * PACK
 PASSES = K // K_PASS
 GROUPS = N // K_PASS
+QUADRANT = 32
+QUADRANTS = P // QUADRANT
+SCALE_ROWS = 4
+PER_COLUMN = 16
+BANKS = 8
 HALF = 512
 QUARTER = 256
-QUADRANT = 32
+LINE = 4
 MOVED_ROWS = 112
 
 
@@ -45,90 +50,98 @@ def tile_list_pasta_humidity_features_kernel(
         scale_window = slot("slot_a", [P, T], U8, "scale_window")
         nc.gpsimd.memset(scale_window[:, : T // 2].bitcast(I32), 0)
         nc.vector.memset(scale_window[:, T // 2 :].bitcast(I32), 0)
-        w2s_raw = keep.tile([P, PASSES, H], U8, name="w2s_raw", align_bytes=64)
-        nc.vector.memset(w2s_raw[:].bitcast(I32), 0)
-        moved = [keep.tile([P, S], U8, name="moved%d" % a, align_bytes=64) for a in range(1, PASSES)]
-        for plane in moved:
-            nc.gpsimd.memset(plane[:].bitcast(I32), 0)
+        w2_scale_rows = keep.tile([P, PASSES, H], U8, name="w2_scale_rows", align_bytes=64)
+        nc.vector.memset(w2_scale_rows[:].bitcast(I32), 0)
+        moved_scales = [keep.tile([P, S], U8, name="moved_scales%d" % a, align_bytes=64) for a in range(1, PASSES)]
+        for scales in moved_scales:
+            nc.gpsimd.memset(scales[:].bitcast(I32), 0)
 
-        def load_words(a, tag):
+        def load_table_words(a, tag):
             window = slot(tag, [P, T], I32, "word_window%d" % a)
             nc.sync.dma_start(window[:], tab_words[a].rearrange("p t i -> p (t i)").bitcast(I32))
             return window
 
         def load_w1(a, tag):
-            raw = slot(tag, [P, PACK, H], F32, "w1_raw%d" % a)
-            nc.sync.dma_start(raw[:], w1[a * K_PASS : (a + 1) * K_PASS, :].rearrange("(p j) c -> p j c", j=PACK))
-            return raw
+            rows = slot(tag, [P, PACK, H], F32, "w1_rows%d" % a)
+            nc.sync.dma_start(rows[:], w1[a * K_PASS : (a + 1) * K_PASS, :].rearrange("(p j) c -> p j c", j=PACK))
+            return rows
 
-        offs_t = keep.tile([P, S // 16], U16, name="offs_t")
+        offs_t = keep.tile([P, S // PER_COLUMN], U16, name="offs_t")
         nc.sync.dma_start(offs_t[:], offs)
-        word_window = [load_words(0, "slot_d")]
-        for q in range(4):
+        word_windows = [load_table_words(0, "word_window0")]
+        for q in range(QUADRANTS):
             nc.sync.dma_start(
-                scale_window[QUADRANT * q : QUADRANT * q + 4 * PASSES, :].bitcast(I32),
-                tab_scales[:, 4 * q : 4 * q + 4, :].bitcast(I32),
+                scale_window[QUADRANT * q : QUADRANT * q + SCALE_ROWS * PASSES, :].bitcast(I32),
+                tab_scales[:, SCALE_ROWS * q : SCALE_ROWS * (q + 1), :].bitcast(I32),
             )
-        w2w_raw = keep.tile([P, PASSES, 2 * H], U8, name="w2w_raw", align_bytes=64)
-        nc.sync.dma_start(w2w_raw[:].bitcast(I32), w2_words.rearrange("a p n -> p a n").bitcast(I32))
-        pos1_t = keep.tile([P, M // 16], U16, name="pos1_t")
+        w2_word_rows = keep.tile([P, PASSES, 2 * H], U8, name="w2_word_rows", align_bytes=64)
+        nc.sync.dma_start(w2_word_rows[:].bitcast(I32), w2_words.rearrange("a p n -> p a n").bitcast(I32))
+        pos1_t = keep.tile([P, M // PER_COLUMN], U16, name="pos1_t")
         nc.sync.dma_start(pos1_t[:], pos1)
-        pos2_t = keep.tile([P, M // 16], U16, name="pos2_t")
+        pos2_t = keep.tile([P, M // PER_COLUMN], U16, name="pos2_t")
         nc.sync.dma_start(pos2_t[:], pos2)
         gain_t = keep.tile([P, PACK], F32, name="gain_t")
         nc.sync.dma_start(gain_t[:], gain.rearrange("(p t) -> p t", t=PACK))
-        word_window.append(load_words(1, "slot_e"))
-        for q in range(4):
+        word_windows.append(load_table_words(1, "slot_e"))
+        for q in range(QUADRANTS):
             nc.sync.dma_start(
-                w2s_raw[QUADRANT * q : QUADRANT * q + 4, :, :].bitcast(I32),
-                w2_scales[:, 4 * q : 4 * q + 4, :].rearrange("a r n -> r a n").bitcast(I32),
+                w2_scale_rows[QUADRANT * q : QUADRANT * q + SCALE_ROWS, :, :].bitcast(I32),
+                w2_scales[:, SCALE_ROWS * q : SCALE_ROWS * (q + 1), :].rearrange("a r n -> r a n").bitcast(I32),
             )
-        w1_raw = [load_w1(0, "slot_b")]
+        w1_rows = [load_w1(0, "slot_b")]
 
         picked_scales = keep.tile([P, S], U8, name="picked_scales", align_bytes=64)
         nc.vector.tensor_copy(picked_scales[:], scale_window[:].indirect(offs_t[:]))
         for a in range(1, PASSES):
             nc.sync.dma_start(
-                moved[a - 1][0:MOVED_ROWS, :].bitcast(I32),
-                picked_scales[4 * a : 4 * a + MOVED_ROWS, :].bitcast(I32),
+                moved_scales[a - 1][0:MOVED_ROWS, :].bitcast(I32),
+                picked_scales[SCALE_ROWS * a : SCALE_ROWS * a + MOVED_ROWS, :].bitcast(I32),
             )
-        v_scales = [picked_scales] + moved
-        word_window.append(load_words(2, "slot_a"))
-        w2w = slot("slot_f", [P, PASSES, 2 * H], U8, "w2w")
+        v_scales = [picked_scales] + moved_scales
+        word_windows.append(load_table_words(2, "slot_a"))
+
+        w2_codes = slot("slot_f", [P, PASSES, 2 * H], U8, "w2_codes")
         for a in range(PASSES):
             nc.vector.tensor_copy(
-                out=w2w[:, a, :].rearrange("p (t m e) -> p t m e", t=PACK, e=2),
-                in_=w2w_raw[:, a, :].rearrange("p (m t e) -> p t m e", t=PACK, e=2),
+                out=w2_codes[:, a, :].rearrange("p (t m e) -> p t m e", t=PACK, e=2),
+                in_=w2_word_rows[:, a, :].rearrange("p (m t e) -> p t m e", t=PACK, e=2),
             )
-        w2s = keep.tile([P, PASSES, H], U8, name="w2s", align_bytes=64)
+        w2_dealt_scales = keep.tile([P, PASSES, H], U8, name="w2_dealt_scales", align_bytes=64)
         for a in range(PASSES):
             nc.vector.tensor_copy(
-                out=w2s[:, a, :].rearrange("p (t m) -> p t m", t=PACK),
-                in_=w2s_raw[:, a, :].rearrange("p (m t) -> p t m", t=PACK),
+                out=w2_dealt_scales[:, a, :].rearrange("p (t m) -> p t m", t=PACK),
+                in_=w2_scale_rows[:, a, :].rearrange("p (m t) -> p t m", t=PACK),
             )
 
         def pick_words(a):
-            window = word_window[a][:].bitcast(U32)
-            halves = []
-            for hf in range(2):
+            window = word_windows[a][:].bitcast(U32)
+            picked = []
+            for hf in range(S // HALF):
                 words = slot("words%d_%d" % (a, hf), [P, HALF], U32, "v_words%d_%d" % (a, hf))
-                nc.vector.tensor_copy(words[:], window.indirect(offs_t[:, hf * HALF // 16 : (hf + 1) * HALF // 16]))
-                halves.append(words)
-            return halves
+                entries = offs_t[:, hf * HALF // PER_COLUMN : (hf + 1) * HALF // PER_COLUMN]
+                nc.vector.tensor_copy(words[:], window.indirect(entries))
+                picked.append(words)
+            return picked
+
+        def deal_views(rounded, rows):
+            return (
+                rounded[:].rearrange("p (u e m j) -> p u m j e", u=2, e=2, j=PACK),
+                rows[:].rearrange("p j (m u e) -> p u m j e", u=2, e=2),
+            )
 
         w1_codes = [slot("w1_codes%d" % a, [P, H], U32, "w1_codes%d" % a) for a in range(PASSES)]
         w1_scales = [keep.tile([P, H], U8, name="w1_scales%d" % a, align_bytes=64) for a in range(PASSES)]
 
-        def quantise_w1(a, tag, parts):
+        def quantise_w1(a, tag):
             rounded = slot(tag, [P, PACK * H], BF16, "w1_rounded%d" % a)
-            dealt = rounded[:].rearrange("p (u e m j) -> p u m j e", u=2, e=2, j=PACK)
-            rows = w1_raw[a][:].rearrange("p j (m u e) -> p u m j e", u=2, e=2)
-            if parts == 1:
+            dealt, rows = deal_views(rounded, w1_rows[a])
+            if a < PASSES - 1:
+                width = H
                 nc.vector.tensor_copy(out=dealt, in_=rows)
             else:
+                width = H // 2
                 for u in range(2):
                     nc.vector.tensor_copy(out=dealt[:, u, :, :, :], in_=rows[:, u, :, :, :])
-            width = H // parts
             for c0 in range(0, H, width):
                 nc.vector.quantize_mx(
                     out=w1_codes[a][:, c0 : c0 + width].bitcast(FP8X4),
@@ -137,37 +150,37 @@ def tile_list_pasta_humidity_features_kernel(
                 )
 
         v_words = [pick_words(0), pick_words(1)]
-        w1_raw.append(load_w1(1, "slot_e"))
-        quantise_w1(0, "slot_g", 1)
-        w1_raw.append(load_w1(2, "slot_b"))
+        w1_rows.append(load_w1(1, "slot_e"))
+        quantise_w1(0, "slot_g")
+        w1_rows.append(load_w1(2, "slot_b"))
         v_words.append(pick_words(2))
 
-        b_banks = [[bank(PACK * hf + t, [P, HALF]) for t in range(PACK)] for hf in range(2)]
+        b_banks = [[bank(PACK * hf + t, [P, HALF]) for t in range(PACK)] for hf in range(S // HALF)]
         for a in range(PASSES):
-            for hf in range(2):
+            for hf in range(S // HALF):
                 cols = slice(hf * HALF, (hf + 1) * HALF)
                 for t in range(PACK):
                     nc.tensor.matmul_mx(
                         out=b_banks[hf][t][:],
-                        lhsT=w2w[:, a, 2 * P * t : 2 * P * (t + 1)].bitcast(FP4X4),
-                        lhsT_scale=w2s[:, a, P * t : P * (t + 1)],
+                        lhsT=w2_codes[:, a, 2 * P * t : 2 * P * (t + 1)].bitcast(FP4X4),
+                        lhsT_scale=w2_dealt_scales[:, a, P * t : P * (t + 1)],
                         rhs=v_words[a][hf][:].bitcast(FP8X4),
                         rhs_scale=v_scales[a][:, cols],
                         start=(a == 0),
                         stop=(a == PASSES - 1),
                     )
         gain_b = keep.tile([P, PACK, S], F32, name="gain_b")
-        for hf in range(2):
+        for hf in range(S // HALF):
             for t in range(PACK):
                 nc.scalar.activation(
                     gain_b[:, t, hf * HALF : (hf + 1) * HALF], b_banks[hf][t][:], ACT.Copy, scale=gain_t[:, t : t + 1]
                 )
 
-        quantise_w1(1, "slot_h", 1)
-        quantise_w1(2, "slot_i", 2)
+        quantise_w1(1, "w1_rounded1")
+        quantise_w1(2, "w1_rounded2")
 
         a_banks = []
-        for hf in range(2):
+        for hf in range(S // HALF):
             cols = slice(hf * HALF, (hf + 1) * HALF)
             a_banks.append([bank(PACK * hf + t, [P, HALF]) for t in range(PACK)])
             for a in range(PASSES):
@@ -182,31 +195,35 @@ def tile_list_pasta_humidity_features_kernel(
                         stop=(a == PASSES - 1),
                     )
 
-        w3_raw, level = [], []
+        w3_rows, level = [], []
         w3_tags = ["slot_g", "words0_1"]
         level_tags = [["slot_a", "slot_f", "slot_e", "slot_b"], ["words1_1", "words2_1", "w1_codes2", "w1_codes1"]]
         for g in range(GROUPS):
-            raw = slot(w3_tags[g], [P, PACK, K_PASS], F32, "w3_raw%d" % g)
-            nc.sync.dma_start(raw[:], w3[:, g * K_PASS : (g + 1) * K_PASS].rearrange("(p j) c -> p j c", j=PACK))
-            w3_raw.append(raw)
-            rows = lowest[g * K_PASS : (g + 1) * K_PASS, :].rearrange("(p t) s -> p t s", t=PACK)
+            rows = slot(w3_tags[g], [P, PACK, K_PASS], F32, "w3_rows%d" % g)
+            nc.sync.dma_start(rows[:], w3[:, g * K_PASS : (g + 1) * K_PASS].rearrange("(p j) c -> p j c", j=PACK))
+            w3_rows.append(rows)
+            lowest_rows = lowest[g * K_PASS : (g + 1) * K_PASS, :].rearrange("(p t) s -> p t s", t=PACK)
             level.append([])
             for t in range(PACK):
-                lv = slot(level_tags[g][t], [P, S], F32, "level%d_%d" % (g, t))
-                nc.sync.dma_start(lv[:], rows[:, t, :])
-                level[g].append(lv)
+                level_rows = slot(level_tags[g][t], [P, S], F32, "level%d_%d" % (g, t))
+                nc.sync.dma_start(level_rows[:], lowest_rows[:, t, :])
+                level[g].append(level_rows)
 
         w3_codes = keep.tile([P, N], U32, name="w3_codes", align_bytes=64)
         w3_scales = keep.tile([P, N], U8, name="w3_scales", align_bytes=64)
 
         def quantise_w3(g, copy, tag):
             rounded = ring.tile([P, PACK * K_PASS], BF16, name="w3_rounded", tag=tag, align_bytes=64)
-            copy(
-                out=rounded[:].rearrange("p (u e m j) -> p u m j e", u=2, e=2, j=PACK),
-                in_=w3_raw[g][:].rearrange("p j (m u e) -> p u m j e", u=2, e=2),
-            )
+            dealt, rows = deal_views(rounded, w3_rows[g])
+            copy(out=dealt, in_=rows)
             cols = slice(g * K_PASS, (g + 1) * K_PASS)
             nc.vector.quantize_mx(out=w3_codes[:, cols].bitcast(FP8X4), scales=w3_scales[:, cols], in_=rounded[:])
+
+        def interleave(copy, rounded, rows):
+            copy(
+                out=rounded.rearrange("p (c i t) -> p c t i", i=LINE, t=PACK),
+                in_=rows.rearrange("p t (c i) -> p c t i", i=LINE),
+            )
 
         quantise_w3(0, nc.vector.tensor_copy, "w3_rounded")
 
@@ -214,11 +231,11 @@ def tile_list_pasta_humidity_features_kernel(
         h_scales = keep.tile([P, S], U8, name="h_scales", align_bytes=64)
 
         def second_product(out, g, t, cols):
-            wcols = slice(g * K_PASS + t * P, g * K_PASS + (t + 1) * P)
+            places = slice(g * K_PASS + t * P, g * K_PASS + (t + 1) * P)
             nc.tensor.matmul_mx(
                 out=out,
-                lhsT=w3_codes[:, wcols].bitcast(FP8X4),
-                lhsT_scale=w3_scales[:, wcols],
+                lhsT=w3_codes[:, places].bitcast(FP8X4),
+                lhsT_scale=w3_scales[:, places],
                 rhs=h_codes[:, cols].bitcast(FP8X4),
                 rhs_scale=h_scales[:, cols],
                 start=True,
@@ -226,7 +243,7 @@ def tile_list_pasta_humidity_features_kernel(
             )
 
         for qt in range(S // QUARTER):
-            hf, part = divmod(qt, 2)
+            hf, part = divmod(qt, HALF // QUARTER)
             cols = slice(qt * QUARTER, (qt + 1) * QUARTER)
             h_rows = ring.tile([P, PACK, QUARTER], F32, name="h_rows", align_bytes=64)
             size = ring.tile([P, PACK, QUARTER], F32, name="size")
@@ -240,19 +257,15 @@ def tile_list_pasta_humidity_features_kernel(
                     h_rows[:, t, :], root[:, t, :], gain_t[:, t : t + 1], gain_b[:, t, cols], ALU.mult, ALU.subtract
                 )
             h_rounded = ring.tile([P, PACK * QUARTER], BF16, name="h_rounded", align_bytes=64)
-            copy = nc.vector.tensor_copy if qt in (0, S // QUARTER - 1) else nc.scalar.copy
-            copy(
-                out=h_rounded[:].rearrange("p (c i t) -> p c t i", i=4, t=PACK),
-                in_=h_rows[:].rearrange("p t (c i) -> p c t i", i=4),
-            )
+            interleave(nc.vector.tensor_copy if qt == 0 else nc.scalar.copy, h_rounded[:], h_rows[:])
             nc.vector.quantize_mx(out=h_codes[:, cols].bitcast(FP8X4), scales=h_scales[:, cols], in_=h_rounded[:])
             for pair in range(2):
                 both = bank(2 * part + pair, [P, 2, QUARTER])
                 for e in range(2):
                     second_product(both[:, e, :], 0, 2 * pair + e, cols)
                 for e in range(2):
-                    lv = level[0][2 * pair + e]
-                    nc.vector.tensor_tensor(lv[:, cols], both[:, e, :], lv[:, cols], ALU.max)
+                    level_rows = level[0][2 * pair + e]
+                    nc.vector.tensor_tensor(level_rows[:, cols], both[:, e, :], level_rows[:, cols], ALU.max)
 
         quantise_w3(1, nc.scalar.copy, "h_rows")
 
@@ -262,51 +275,44 @@ def tile_list_pasta_humidity_features_kernel(
         y_scales = [keep.tile([P, M], U8, name="y_scales%d" % g, align_bytes=64) for g in range(GROUPS)]
 
         def raise_level(g, t):
-            lv = level[g][t]
-            for hf in range(2):
+            level_rows = level[g][t]
+            for hf in range(S // HALF):
                 cols = slice(hf * HALF, (hf + 1) * HALF)
-                acc = bank((2 * t + hf + PACK) % 8, [P, HALF])
-                second_product(acc[:], g, t, cols)
-                nc.vector.tensor_tensor(lv[:, cols], acc[:], lv[:, cols], ALU.max)
+                product = bank((2 * t + hf + PACK) % BANKS, [P, HALF])
+                second_product(product[:], g, t, cols)
+                nc.vector.tensor_tensor(level_rows[:, cols], product[:], level_rows[:, cols], ALU.max)
 
         def pick_core(g, t, m0, m1):
             core = ring.tile([P, m1 - m0], F32, name="core", bufs=3)
-            nc.vector.tensor_copy(core[:], level[g][t][:].indirect(pos1_t[:, m0 // 16 : m1 // 16]))
+            nc.vector.tensor_copy(core[:], level[g][t][:].indirect(pos1_t[:, m0 // PER_COLUMN : m1 // PER_COLUMN]))
             return core
 
-        def planes(g, m0, m1, copy):
-            copy(
-                out=y_rounded[g][:, PACK * m0 : PACK * m1].rearrange("p (c i t) -> p c t i", i=4, t=PACK),
-                in_=y_tiles[g][:, :, m0:m1].rearrange("p t (c i) -> p c t i", i=4),
-            )
-            nc.vector.quantize_mx(
-                out=y_codes[g][:, m0:m1].bitcast(FP8X4),
-                scales=y_scales[g][:, m0:m1],
-                in_=y_rounded[g][:, PACK * m0 : PACK * m1],
-            )
-            nc.sync.dma_start(
-                out_1[g, :, m0:m1, :].rearrange("p m t -> p (m t)").bitcast(I32), y_codes[g][:, m0:m1].bitcast(I32)
-            )
-            if m1 == M:
-                for q in range(4):
-                    queue = nc.sync if q % 2 == 0 else nc.scalar
-                    queue.dma_start(
-                        out_2[g, 4 * q : 4 * q + 4, :].bitcast(I32), y_scales[g][32 * q : 32 * q + 4, :].bitcast(I32)
-                    )
+        def round_y(g, m0, m1, copy):
+            interleave(copy, y_rounded[g][:, PACK * m0 : PACK * m1], y_tiles[g][:, :, m0:m1])
+
+        def store_quantised_y(g, queues):
+            nc.vector.quantize_mx(out=y_codes[g][:].bitcast(FP8X4), scales=y_scales[g][:], in_=y_rounded[g][:])
+            nc.sync.dma_start(out_1[g].rearrange("p m t -> p (m t)").bitcast(I32), y_codes[g][:].bitcast(I32))
+            for q in range(QUADRANTS):
+                queues[q % len(queues)].dma_start(
+                    out_2[g, SCALE_ROWS * q : SCALE_ROWS * (q + 1), :].bitcast(I32),
+                    y_scales[g][QUADRANT * q : QUADRANT * q + SCALE_ROWS, :].bitcast(I32),
+                )
 
         def add_surface(g, t, m0, m1, core):
-            pair_sum = ring.tile([P, m1 - m0], F32, name="pair_sum")
-            nc.vector.tensor_tensor(
-                pair_sum[:], level[g][t][:].indirect(pos2_t[:, m0 // 16 : m1 // 16]), core[:], ALU.add
-            )
+            pair_sum = ring.tile([P, m1 - m0], F32, name="pair_sum", bufs=4)
+            surface = level[g][t][:].indirect(pos2_t[:, m0 // PER_COLUMN : m1 // PER_COLUMN])
+            nc.vector.tensor_tensor(pair_sum[:], surface, core[:], ALU.add)
             nc.scalar.activation(y_tiles[g][:, t, m0:m1], pair_sum[:], ACT.Abs)
-            y_rows = out_0[g * K_PASS : (g + 1) * K_PASS, :].rearrange("(p t) m -> p t m", t=PACK)
-            nc.sync.dma_start(y_rows[:, t, m0:m1], y_tiles[g][:, t, m0:m1])
-            if t == PACK - 1:
-                planes(g, m0, m1, nc.vector.tensor_copy if (g == GROUPS - 1 and m1 == M) else nc.scalar.copy)
+            out_rows = out_0[g * K_PASS : (g + 1) * K_PASS, :].rearrange("(p t) m -> p t m", t=PACK)
+            nc.sync.dma_start(out_rows[:, t, m0:m1], y_tiles[g][:, t, m0:m1])
+            if (g, t) == (0, PACK - 1):
+                round_y(g, 0, M, nc.scalar.copy)
+                store_quantised_y(g, [nc.sync])
 
+        halves = [(0, M // 2), (M // 2, M)]
         pieces = [(g, t, 0, M) for g in range(GROUPS) for t in range(PACK)][:-1]
-        pieces.extend([(GROUPS - 1, PACK - 1, 0, M // 2), (GROUPS - 1, PACK - 1, M // 2, M)])
+        pieces.extend([(GROUPS - 1, PACK - 1, m0, m1) for m0, m1 in halves])
         waiting = None
         for i, (g, t, m0, m1) in enumerate(pieces):
             if PACK <= i + 1 < GROUPS * PACK:
@@ -316,3 +322,7 @@ def tile_list_pasta_humidity_features_kernel(
                 add_surface(*waiting)
             waiting = (g, t, m0, m1, core)
         add_surface(*waiting)
+
+        for m0, m1 in halves:
+            round_y(GROUPS - 1, m0, m1, nc.vector.tensor_copy)
+        store_quantised_y(GROUPS - 1, [nc.sync, nc.scalar])

from contextlib import ExitStack

import concourse.mybir as mybir

K, H, N, T, S, M = 1536, 512, 1024, 4096, 1024, 512
FLOPS = 2 * K * H * S * 2 + 2 * H * N * S

F32 = mybir.dt.float32
BF16 = mybir.dt.bfloat16
I32 = mybir.dt.int32
U32 = mybir.dt.uint32
U16 = mybir.dt.uint16
U8 = mybir.dt.uint8
FP8X4 = mybir.dt.float8_e4m3fn_x4
FP4X4 = mybir.dt.float4_e2m1fn_x4
ACT = mybir.ActivationFunctionType
ALU = mybir.AluOpType

P = 128
PACK = 4
K_PASS = P * PACK
PASSES = K // K_PASS
GROUPS = N // K_PASS
QUADRANT = 32
QUADRANTS = P // QUADRANT
SCALE_ROWS = 4
PER_COLUMN = 16
BANKS = 8
HALF = 512
QUARTER = 256
LINE = 4
MOVED_ROWS = 112


def tile_list_pasta_humidity_features_kernel(
    tc, tab_words, tab_scales, offs, pos1, pos2, w1, w2_words, w2_scales, gain, w3, lowest, out_0, out_1, out_2
):
    nc = tc.nc
    with ExitStack() as ctx:
        keep = ctx.enter_context(tc.tile_pool(name="keep", bufs=1))
        ring = ctx.enter_context(tc.tile_pool(name="ring", bufs=2))
        psum = ctx.enter_context(tc.psum_pool(name="psum", bufs=1))

        def bank(b, shape):
            return psum.tile(shape, F32, name="bank%d" % b, tag="bank%d" % b)

        def slot(tag, shape, dtype, name):
            return keep.tile(shape, dtype, name=name, tag=tag, align_bytes=64)

        scale_window = slot("slot_a", [P, T], U8, "scale_window")
        nc.gpsimd.memset(scale_window[:, : T // 2].bitcast(I32), 0)
        nc.vector.memset(scale_window[:, T // 2 :].bitcast(I32), 0)
        w2_scale_rows = keep.tile([P, PASSES, H], U8, name="w2_scale_rows", align_bytes=64)
        nc.vector.memset(w2_scale_rows[:].bitcast(I32), 0)
        moved_scales = [keep.tile([P, S], U8, name="moved_scales%d" % a, align_bytes=64) for a in range(1, PASSES)]
        for scales in moved_scales:
            nc.gpsimd.memset(scales[:].bitcast(I32), 0)

        def load_table_words(a, tag):
            window = slot(tag, [P, T], I32, "word_window%d" % a)
            nc.sync.dma_start(window[:], tab_words[a].rearrange("p t i -> p (t i)").bitcast(I32))
            return window

        def load_w1(a, tag):
            rows = slot(tag, [P, PACK, H], F32, "w1_rows%d" % a)
            nc.sync.dma_start(rows[:], w1[a * K_PASS : (a + 1) * K_PASS, :].rearrange("(p j) c -> p j c", j=PACK))
            return rows

        offs_t = keep.tile([P, S // PER_COLUMN], U16, name="offs_t")
        nc.sync.dma_start(offs_t[:], offs)
        word_windows = [load_table_words(0, "word_window0")]
        for q in range(QUADRANTS):
            nc.sync.dma_start(
                scale_window[QUADRANT * q : QUADRANT * q + SCALE_ROWS * PASSES, :].bitcast(I32),
                tab_scales[:, SCALE_ROWS * q : SCALE_ROWS * (q + 1), :].bitcast(I32),
            )
        w2_word_rows = keep.tile([P, PASSES, 2 * H], U8, name="w2_word_rows", align_bytes=64)
        nc.sync.dma_start(w2_word_rows[:].bitcast(I32), w2_words.rearrange("a p n -> p a n").bitcast(I32))
        pos1_t = keep.tile([P, M // PER_COLUMN], U16, name="pos1_t")
        nc.sync.dma_start(pos1_t[:], pos1)
        pos2_t = keep.tile([P, M // PER_COLUMN], U16, name="pos2_t")
        nc.sync.dma_start(pos2_t[:], pos2)
        gain_t = keep.tile([P, PACK], F32, name="gain_t")
        nc.sync.dma_start(gain_t[:], gain.rearrange("(p t) -> p t", t=PACK))
        word_windows.append(load_table_words(1, "slot_e"))
        for q in range(QUADRANTS):
            nc.sync.dma_start(
                w2_scale_rows[QUADRANT * q : QUADRANT * q + SCALE_ROWS, :, :].bitcast(I32),
                w2_scales[:, SCALE_ROWS * q : SCALE_ROWS * (q + 1), :].rearrange("a r n -> r a n").bitcast(I32),
            )
        w1_rows = [load_w1(0, "slot_b")]

        picked_scales = keep.tile([P, S], U8, name="picked_scales", align_bytes=64)
        nc.vector.tensor_copy(picked_scales[:], scale_window[:].indirect(offs_t[:]))
        for a in range(1, PASSES):
            nc.sync.dma_start(
                moved_scales[a - 1][0:MOVED_ROWS, :].bitcast(I32),
                picked_scales[SCALE_ROWS * a : SCALE_ROWS * a + MOVED_ROWS, :].bitcast(I32),
            )
        v_scales = [picked_scales] + moved_scales
        word_windows.append(load_table_words(2, "slot_a"))

        w2_codes = slot("slot_f", [P, PASSES, 2 * H], U8, "w2_codes")
        for a in range(PASSES):
            nc.vector.tensor_copy(
                out=w2_codes[:, a, :].rearrange("p (t m e) -> p t m e", t=PACK, e=2),
                in_=w2_word_rows[:, a, :].rearrange("p (m t e) -> p t m e", t=PACK, e=2),
            )
        w2_dealt_scales = keep.tile([P, PASSES, H], U8, name="w2_dealt_scales", align_bytes=64)
        for a in range(PASSES):
            nc.vector.tensor_copy(
                out=w2_dealt_scales[:, a, :].rearrange("p (t m) -> p t m", t=PACK),
                in_=w2_scale_rows[:, a, :].rearrange("p (m t) -> p t m", t=PACK),
            )

        def pick_words(a):
            window = word_windows[a][:].bitcast(U32)
            picked = []
            for hf in range(S // HALF):
                words = slot("words%d_%d" % (a, hf), [P, HALF], U32, "v_words%d_%d" % (a, hf))
                entries = offs_t[:, hf * HALF // PER_COLUMN : (hf + 1) * HALF // PER_COLUMN]
                nc.vector.tensor_copy(words[:], window.indirect(entries))
                picked.append(words)
            return picked

        def deal_views(rounded, rows):
            return (
                rounded[:].rearrange("p (u e m j) -> p u m j e", u=2, e=2, j=PACK),
                rows[:].rearrange("p j (m u e) -> p u m j e", u=2, e=2),
            )

        w1_codes = [slot("w1_codes%d" % a, [P, H], U32, "w1_codes%d" % a) for a in range(PASSES)]
        w1_scales = [keep.tile([P, H], U8, name="w1_scales%d" % a, align_bytes=64) for a in range(PASSES)]

        def quantise_w1(a, tag):
            rounded = slot(tag, [P, PACK * H], BF16, "w1_rounded%d" % a)
            dealt, rows = deal_views(rounded, w1_rows[a])
            if a < PASSES - 1:
                width = H
                nc.vector.tensor_copy(out=dealt, in_=rows)
            else:
                width = H // 2
                for u in range(2):
                    nc.vector.tensor_copy(out=dealt[:, u, :, :, :], in_=rows[:, u, :, :, :])
            for c0 in range(0, H, width):
                nc.vector.quantize_mx(
                    out=w1_codes[a][:, c0 : c0 + width].bitcast(FP8X4),
                    scales=w1_scales[a][:, c0 : c0 + width],
                    in_=rounded[:, PACK * c0 : PACK * (c0 + width)],
                )

        v_words = [pick_words(0), pick_words(1)]
        w1_rows.append(load_w1(1, "slot_e"))
        quantise_w1(0, "slot_g")
        w1_rows.append(load_w1(2, "slot_b"))
        v_words.append(pick_words(2))

        b_banks = [[bank(PACK * hf + t, [P, HALF]) for t in range(PACK)] for hf in range(S // HALF)]
        for a in range(PASSES):
            for hf in range(S // HALF):
                cols = slice(hf * HALF, (hf + 1) * HALF)
                for t in range(PACK):
                    nc.tensor.matmul_mx(
                        out=b_banks[hf][t][:],
                        lhsT=w2_codes[:, a, 2 * P * t : 2 * P * (t + 1)].bitcast(FP4X4),
                        lhsT_scale=w2_dealt_scales[:, a, P * t : P * (t + 1)],
                        rhs=v_words[a][hf][:].bitcast(FP8X4),
                        rhs_scale=v_scales[a][:, cols],
                        start=(a == 0),
                        stop=(a == PASSES - 1),
                    )
        gain_b = keep.tile([P, PACK, S], F32, name="gain_b")
        for hf in range(S // HALF):
            for t in range(PACK):
                nc.scalar.activation(
                    gain_b[:, t, hf * HALF : (hf + 1) * HALF], b_banks[hf][t][:], ACT.Copy, scale=gain_t[:, t : t + 1]
                )

        quantise_w1(1, "w1_rounded1")
        quantise_w1(2, "w1_rounded2")

        a_banks = []
        for hf in range(S // HALF):
            cols = slice(hf * HALF, (hf + 1) * HALF)
            a_banks.append([bank(PACK * hf + t, [P, HALF]) for t in range(PACK)])
            for a in range(PASSES):
                for t in range(PACK):
                    nc.tensor.matmul_mx(
                        out=a_banks[hf][t][:],
                        lhsT=w1_codes[a][:, P * t : P * (t + 1)].bitcast(FP8X4),
                        lhsT_scale=w1_scales[a][:, P * t : P * (t + 1)],
                        rhs=v_words[a][hf][:].bitcast(FP8X4),
                        rhs_scale=v_scales[a][:, cols],
                        start=(a == 0),
                        stop=(a == PASSES - 1),
                    )

        w3_rows, level = [], []
        w3_tags = ["slot_g", "words0_1"]
        level_tags = [["slot_a", "slot_f", "slot_e", "slot_b"], ["words1_1", "words2_1", "w1_codes2", "w1_codes1"]]
        for g in range(GROUPS):
            rows = slot(w3_tags[g], [P, PACK, K_PASS], F32, "w3_rows%d" % g)
            nc.sync.dma_start(rows[:], w3[:, g * K_PASS : (g + 1) * K_PASS].rearrange("(p j) c -> p j c", j=PACK))
            w3_rows.append(rows)
            lowest_rows = lowest[g * K_PASS : (g + 1) * K_PASS, :].rearrange("(p t) s -> p t s", t=PACK)
            level.append([])
            for t in range(PACK):
                level_rows = slot(level_tags[g][t], [P, S], F32, "level%d_%d" % (g, t))
                nc.sync.dma_start(level_rows[:], lowest_rows[:, t, :])
                level[g].append(level_rows)

        w3_codes = keep.tile([P, N], U32, name="w3_codes", align_bytes=64)
        w3_scales = keep.tile([P, N], U8, name="w3_scales", align_bytes=64)

        def quantise_w3(g, copy, tag):
            rounded = ring.tile([P, PACK * K_PASS], BF16, name="w3_rounded", tag=tag, align_bytes=64)
            dealt, rows = deal_views(rounded, w3_rows[g])
            copy(out=dealt, in_=rows)
            cols = slice(g * K_PASS, (g + 1) * K_PASS)
            nc.vector.quantize_mx(out=w3_codes[:, cols].bitcast(FP8X4), scales=w3_scales[:, cols], in_=rounded[:])

        def interleave(copy, rounded, rows):
            copy(
                out=rounded.rearrange("p (c i t) -> p c t i", i=LINE, t=PACK),
                in_=rows.rearrange("p t (c i) -> p c t i", i=LINE),
            )

        quantise_w3(0, nc.vector.tensor_copy, "w3_rounded")

        h_codes = keep.tile([P, S], U32, name="h_codes", align_bytes=64)
        h_scales = keep.tile([P, S], U8, name="h_scales", align_bytes=64)

        def second_product(out, g, t, cols):
            places = slice(g * K_PASS + t * P, g * K_PASS + (t + 1) * P)
            nc.tensor.matmul_mx(
                out=out,
                lhsT=w3_codes[:, places].bitcast(FP8X4),
                lhsT_scale=w3_scales[:, places],
                rhs=h_codes[:, cols].bitcast(FP8X4),
                rhs_scale=h_scales[:, cols],
                start=True,
                stop=True,
            )

        for qt in range(S // QUARTER):
            hf, part = divmod(qt, HALF // QUARTER)
            cols = slice(qt * QUARTER, (qt + 1) * QUARTER)
            h_rows = ring.tile([P, PACK, QUARTER], F32, name="h_rows", align_bytes=64)
            size = ring.tile([P, PACK, QUARTER], F32, name="size")
            for t in range(PACK):
                nc.scalar.activation(size[:, t, :], a_banks[hf][t][:, part * QUARTER : (part + 1) * QUARTER], ACT.Abs)
            root = ring.tile([P, PACK, QUARTER], F32, name="root")
            for t in range(0, PACK, 2):
                nc.scalar.activation(root[:, t : t + 2, :], size[:, t : t + 2, :], ACT.Sqrt)
            for t in range(PACK):
                nc.vector.scalar_tensor_tensor(
                    h_rows[:, t, :], root[:, t, :], gain_t[:, t : t + 1], gain_b[:, t, cols], ALU.mult, ALU.subtract
                )
            h_rounded = ring.tile([P, PACK * QUARTER], BF16, name="h_rounded", align_bytes=64)
            interleave(nc.vector.tensor_copy if qt == 0 else nc.scalar.copy, h_rounded[:], h_rows[:])
            nc.vector.quantize_mx(out=h_codes[:, cols].bitcast(FP8X4), scales=h_scales[:, cols], in_=h_rounded[:])
            for pair in range(2):
                both = bank(2 * part + pair, [P, 2, QUARTER])
                for e in range(2):
                    second_product(both[:, e, :], 0, 2 * pair + e, cols)
                for e in range(2):
                    level_rows = level[0][2 * pair + e]
                    nc.vector.tensor_tensor(level_rows[:, cols], both[:, e, :], level_rows[:, cols], ALU.max)

        quantise_w3(1, nc.scalar.copy, "h_rows")

        y_tiles = [keep.tile([P, PACK, M], F32, name="y%d" % g) for g in range(GROUPS)]
        y_rounded = [keep.tile([P, PACK * M], BF16, name="y_rounded%d" % g, align_bytes=64) for g in range(GROUPS)]
        y_codes = [keep.tile([P, M], U32, name="y_codes%d" % g, align_bytes=64) for g in range(GROUPS)]
        y_scales = [keep.tile([P, M], U8, name="y_scales%d" % g, align_bytes=64) for g in range(GROUPS)]

        def raise_level(g, t):
            level_rows = level[g][t]
            for hf in range(S // HALF):
                cols = slice(hf * HALF, (hf + 1) * HALF)
                product = bank((2 * t + hf + PACK) % BANKS, [P, HALF])
                second_product(product[:], g, t, cols)
                nc.vector.tensor_tensor(level_rows[:, cols], product[:], level_rows[:, cols], ALU.max)

        def pick_core(g, t, m0, m1):
            core = ring.tile([P, m1 - m0], F32, name="core", bufs=3)
            nc.vector.tensor_copy(core[:], level[g][t][:].indirect(pos1_t[:, m0 // PER_COLUMN : m1 // PER_COLUMN]))
            return core

        def round_y(g, m0, m1, copy):
            interleave(copy, y_rounded[g][:, PACK * m0 : PACK * m1], y_tiles[g][:, :, m0:m1])

        def store_quantised_y(g, queues):
            nc.vector.quantize_mx(out=y_codes[g][:].bitcast(FP8X4), scales=y_scales[g][:], in_=y_rounded[g][:])
            nc.sync.dma_start(out_1[g].rearrange("p m t -> p (m t)").bitcast(I32), y_codes[g][:].bitcast(I32))
            for q in range(QUADRANTS):
                queues[q % len(queues)].dma_start(
                    out_2[g, SCALE_ROWS * q : SCALE_ROWS * (q + 1), :].bitcast(I32),
                    y_scales[g][QUADRANT * q : QUADRANT * q + SCALE_ROWS, :].bitcast(I32),
                )

        def add_surface(g, t, m0, m1, core):
            pair_sum = ring.tile([P, m1 - m0], F32, name="pair_sum", bufs=4)
            surface = level[g][t][:].indirect(pos2_t[:, m0 // PER_COLUMN : m1 // PER_COLUMN])
            nc.vector.tensor_tensor(pair_sum[:], surface, core[:], ALU.add)
            nc.scalar.activation(y_tiles[g][:, t, m0:m1], pair_sum[:], ACT.Abs)
            out_rows = out_0[g * K_PASS : (g + 1) * K_PASS, :].rearrange("(p t) m -> p t m", t=PACK)
            nc.sync.dma_start(out_rows[:, t, m0:m1], y_tiles[g][:, t, m0:m1])
            if (g, t) == (0, PACK - 1):
                round_y(g, 0, M, nc.scalar.copy)
                store_quantised_y(g, [nc.sync])

        halves = [(0, M // 2), (M // 2, M)]
        pieces = [(g, t, 0, M) for g in range(GROUPS) for t in range(PACK)][:-1]
        pieces.extend([(GROUPS - 1, PACK - 1, m0, m1) for m0, m1 in halves])
        waiting = None
        for i, (g, t, m0, m1) in enumerate(pieces):
            if PACK <= i + 1 < GROUPS * PACK:
                raise_level(*divmod(i + 1, PACK))
            core = pick_core(g, t, m0, m1)
            if waiting is not None:
                add_surface(*waiting)
            waiting = (g, t, m0, m1, core)
        add_surface(*waiting)

        for m0, m1 in halves:
            round_y(GROUPS - 1, m0, m1, nc.vector.tensor_copy)
        store_quantised_y(GROUPS - 1, [nc.sync, nc.scalar])
